import numpy as np, ml_dtypes
CORES = [113,118,241,246]
N = 4
BF = ml_dtypes.bfloat16
def gentries(a):
    return np.ascontiguousarray(a.reshape(8, 16, -1).transpose(0, 2, 1)).reshape(8, -1)
def gtable(e):
    e = np.asarray(e); return np.ascontiguousarray(e.reshape(8, -1, 16).transpose(0, 2, 1)).reshape(128, -1).astype(np.int32)
V, A, W, M, RO, ST = 2048, 256, 2048, 4096, 3, 8
H, E, Z = V - A, W - 1, M - 1
def parts(rng):
    a = rng.choice(np.array([1, 2, 4, 8]), (8, 16, 1)); b = rng.choice(np.array([15, 63, 255]), (8, 16, 1))
    e = rng.integers(-a, a + 1, (8, 16, W)); c = rng.integers(-b, b + 1, (8, 16, M)); m = rng.integers(0, M, (8, 2, W))
    share = rng.permutation(np.linspace(0.42, 0.7, 8)).reshape(8, 1, 1)
    k = np.where(rng.random((8, 2, M)) < share, rng.integers(0, E, (8, 2, M)), E)
    fill = rng.choice(np.array([0.9, 0.97, 1.0]), (N, 8, 1))
    p = np.where(rng.random((N, 8, V)) < fill, rng.integers(0, E, (N, 8, V)), E)
    return p, e, m, c, k
def lone(rng):
    return np.where(np.arange(2)[:, None] == rng.integers(0, 2, M), rng.integers(0, E, (2, M)), E)
def alike(x):
    return np.ascontiguousarray(np.broadcast_to(x, (N,) + x.shape))
def pack(p, e, m, c, k):
    e[:, :, E] = 0; m[:, :, E] = Z; k[:, :, Z] = E
    return {"todo": np.stack([gtable(a) for a in p]), "eff": alike(e.reshape(128, W).astype(np.float32).astype(BF)),
            "meth": alike((m[:, 0] + 4096 * m[:, 1]).astype(np.int32)), "pre": alike(c.reshape(128, M).astype(np.float32).astype(BF)),
            "kid": alike((k[:, 0] + 4096 * k[:, 1]).astype(np.int32))}
def setup_inputs(rng):
    return pack(*parts(rng))
def setup_inputs_room(rng):
    p, e, m, c, k = parts(rng)
    m = 3 * rng.integers(0, (M - 1) // 3, (8, 2, W)) + np.arange(W) % 3
    k = rng.integers(0, E, (8, 2, M)); one = rng.integers(0, 2, (8, M)); cl = np.arange(M) % 3
    k[:, 0] = np.where((cl == 0) | ((cl == 1) & (one == 0)), E, k[:, 0]); k[:, 1] = np.where((cl == 0) | ((cl == 1) & (one == 1)), E, k[:, 1])
    for q in range(N):
        for g in range(8):
            n = int(rng.choice(np.array([0, 1, H - 1, H, H + 1, V - 1, V, V + 1, 2 * V])))
            if q == 0: n = (V, V + 1, V - 1, H, H + 1, H - 1, 2 * V, 1)[g]
            n2 = int(rng.integers(max(0, n - V), n // 2 + 1)); n1 = n - 2 * n2; n0 = V - n1 - n2
            kinds = rng.permutation(np.repeat(np.array([0, 1, 2]), np.array([n0, n1, n2])))
            t = 3 * rng.integers(0, (W - 1) // 3, V) + kinds
            p[q, g] = np.where((kinds == 0) & (rng.random(V) < 0.3), E, t)
    return pack(p, e, m, c, k)
def setup_inputs_ties(rng):
    p, e, m, c, k = parts(rng)
    e[::2] = rng.integers(-1, 2, (4, 16, W)) * (rng.random((4, 16, W)) < 0.01)
    c[::2] = rng.integers(-2, 3, (4, 16, M))
    m[::2, 1] = np.where(rng.random((4, W)) < 0.3, m[::2, 0], m[::2, 1])
    m[1::2, 1] = m[1::2, 0] ^ 1
    c[1::2, :, 1::2] = c[1::2, :, 0::2]; i = int(rng.integers(0, 16))
    c[1::2, i, 1::2] = rng.integers(-255, 256, (4, M // 2))
    return pack(p, e, m, c, k)
def setup_inputs_ends(rng):
    p, e, m, c, k = parts(rng)
    e[0] = 8; e[1] = -8
    p[:, :2] = rng.integers(0, E, (N, 2, V)); m[:2] = rng.integers(0, Z, (2, 2, W)); c[:2] = rng.integers(-255, 256, (2, 16, M))
    k[0] = lone(rng); k[1] = lone(rng)
    c[2] = rng.choice(np.array([-255, 255, 0]), (16, M))
    p[:, 3] = rng.choice(np.array([0, 1, E - 1, E]), (N, V))
    m[4] = rng.choice(np.array([0, 1, M - 2, Z]), (2, W)); k[4][:, [0, 1, M - 2]] = rng.integers(0, E, (2, 3))
    k[5] = rng.choice(np.array([0, 1, E - 1, E]), (2, M))
    t = rng.permutation(E)[:2]; u = rng.permutation(Z)[:2]
    p[:, 6] = t[0]; m[6, 0, t[0]] = u[0]; m[6, 1, t[0]] = u[1]
    k[6, 0, u[0]] = t[0]; k[6, 1, u[0]] = t[1]; k[6, 0, u[1]] = t[1]; k[6, 1, u[1]] = E
    sg = rng.permutation(np.repeat(np.array([-1, 1]), 8))[:, None]
    e[7] = sg * 8 * (1 - 2 * (np.arange(W) % 2))
    p[:, 7] = 2 * rng.integers(0, E // 2, (N, V)) + (np.arange(N * V).reshape(N, V) >= N * V // 2 + 15)
    m[7, 0] = 2 * rng.integers(0, M // 2, W); m[7, 1] = 2 * rng.integers(0, M // 2 - 1, W) + 1; k[7] = lone(rng)
    lo = rng.integers(-255, 101, (16, M)); hi = rng.integers(-100, 256, (16, M))
    c[7] = np.where(np.arange(M) % 2 == 1, np.where(sg > 0, lo, -255), np.where(sg > 0, 255, hi))
    return pack(p, e, m, c, k)
def setup_inputs_thin(rng):
    p, e, m, c, k = parts(rng); p = rng.integers(0, E, (N, 8, V))
    fill = rng.choice(np.array([0.0, 0.02, 0.3, 1.0]), (N, 8, 1)); o = rng.permutation(8)
    fill[int(rng.integers(0, N))] = 0.0; fill[:, o[0]] = 0.0; fill[:, o[1:3]] = 1.0
    p = np.where(rng.random((N, 8, V)) < fill, p, E); p[:, o[3], :V // 2] = E
    g = int(o[4]); q = int(rng.integers(0, N - 1)); cl = np.arange(M) % 3
    m[g] = 3 * rng.integers(0, (M - 1) // 3, (2, W)) + np.arange(W) % 3
    one = np.arange(2)[:, None] == rng.integers(0, 2, M); leaf = 3 * rng.integers(0, E // 3, (2, M)); go = 3 * rng.integers(0, E // 3, (2, M)) + 2
    k[g] = np.where(cl == 1, leaf, np.where((cl == 2) & one, go, E))
    kinds = np.full(N, 2); kinds[[q - 1, q]] = 1
    p[:, g] = 3 * rng.integers(0, E // 3, (N, V)) + kinds[:, None]; p[(q + 2) % N, g] = E
    return pack(p, e, m, c, k)
def setup_inputs_spread(rng):
    p, e, m, c, k = parts(rng)
    o = np.stack([rng.permutation(E) for g in range(8)]); gi = np.arange(8)
    p = np.where(rng.random((N, 8, V)) < 0.97, o[gi[None, :, None], (E * rng.random((N, 8, V)) ** 4).astype(np.int64)], E)
    k = np.where(k == E, E, o[gi[:, None, None], (E * rng.random((8, 2, M)) ** 3).astype(np.int64)])
    s = rng.choice(np.array([-1, 1]), (8, 16, W)); e = s * np.minimum(8, np.floor(np.exp2(3.2 * rng.random((8, 1, W))) * rng.random((8, 16, W)) + 0.5)).astype(np.int64) * (rng.random((8, 1, W)) > 0.0625)
    s = rng.choice(np.array([-1, 1]), (8, 16, M)); c = s * np.minimum(255, np.floor(np.exp2(8 * rng.random((8, 16, M))))).astype(np.int64)
    w = int(rng.integers(0, 8)); a = rng.choice(np.array([-1, 1]), (16, 1)) * rng.integers(3, 8, (16, 1))
    e[w] = a * np.array([0, 1, -1])[np.arange(W) % 3] + rng.integers(-1, 2, (16, W)); c[w] = rng.integers(-127, 128, (16, M))
    m[w] = rng.integers(0, Z, (2, W)); k[w] = lone(rng)
    kinds = np.zeros((N, V), np.int64); kinds[0::2, V // 2:] = 1; kinds[1::2, :V // 2] = 2
    p[:, w] = 3 * rng.integers(0, E // 3, (N, V)) + kinds
    return pack(p, e, m, c, k)
def check_inputs(d):
    bad = []
    if np.min(d["todo"]) < 0 or np.max(d["todo"]) > E: bad.append("range of todo")
    for nm, hi in (("eff", 8), ("pre", 255)):
        x = np.asarray(d[nm]).astype(np.float32)
        if not np.all((x >= -hi) & (x <= hi) & (x == np.rint(x))): bad.append("whole numbers in range: " + nm)
    for nm, hi in (("meth", Z), ("kid", E)):
        x = np.asarray(d[nm]).astype(np.int64)
        if not np.all((x >= 0) & ((x & 4095) <= hi) & ((x >> 12) <= hi)): bad.append("range of " + nm)
    for nm in ("eff", "meth", "pre", "kid"):
        x = np.asarray(d[nm]).astype(np.float64)
        if not np.all(x == x[:1]): bad.append("not alike on all ranks: " + nm)
    if not np.all(np.asarray(d["eff"])[:, :, E].astype(np.float32) == 0): bad.append("effects of the empty type")
    if not np.all(np.asarray(d["meth"])[:, :, E] == Z + 4096 * Z): bad.append("methods of the empty type")
    if not np.all(np.asarray(d["kid"])[:, :, Z] == E + 4096 * E): bad.append("kids of the empty method")
    return bad
def reference(todo, eff, meth, pre, kid):
    p = np.stack([gentries(a) for a in todo]).astype(np.int64)
    ef = eff.astype(np.float32).astype(np.int64).reshape(N, 8, 16, W); pr = pre.astype(np.float32).astype(np.int64).reshape(N, 8, 16, M)
    me = meth.astype(np.int64); ki = kid.astype(np.int64)
    for rnd in range(RO):
        e = np.take_along_axis(ef, p[:, :, None, :], 3)
        line = np.ascontiguousarray(e.transpose(1, 2, 0, 3)).reshape(8, 16, N * V)
        st = (np.add.accumulate(line, axis=2) - line).reshape(8, 16, N, V).transpose(2, 0, 1, 3)
        m = np.take_along_axis(me, p, 2); m0 = m & 4095; m1 = m >> 12
        c0 = np.add.reduce((st >= np.take_along_axis(pr, m0[:, :, None, :], 3)).astype(np.int64), axis=2)
        c1 = np.add.reduce((st >= np.take_along_axis(pr, m1[:, :, None, :], 3)).astype(np.int64), axis=2)
        k = np.take_along_axis(ki, np.where(c1 > c0, m1, m0), 2)
        kk = np.stack([k & 4095, k >> 12], axis=-1).reshape(N, 8, 2 * V)
        row = np.full((N, 8, V), E, np.int64)
        for a in range(N):
            for g in range(8):
                v = kk[a, g][kk[a, g] != E][:V]; row[a, g, :len(v)] = v
        p = np.concatenate([np.roll(row[:, :, H:], 1, axis=0), row[:, :, :H]], axis=2)
    return {"yp": np.stack([gtable(a) for a in p]).astype(np.float32), "ys": np.ascontiguousarray(st.reshape(N, 128, V)[:, :, ::ST]).astype(np.float32)}

@@ -1,0 +1,522 @@
+from concourse.bass import DstId, RemoteDMATransfer
+from concourse.mybir import AluOpType as Op, ActivationFunctionType as Fn, AxisListType as Ax
+
+V, A, M, RO = 2048, 256, 4096, 3
+EMPTY = V - 1
+NE = 4
+PAD = 16
+WIN = PAD + 5248
+LOW = 1024
+P1V = 640
+ECOL = [16, 288, 544, 800, 1056, 1328, 1584, 1840, 2096]
+PARTS = [(0, 64), (64, 128)]
+
+SCRATCH = {
+    "todo_s": ("sbuf", [128, 128], "int32"), "mi": ("sbuf", [128, 128], "int32"), "m2": ("sbuf", [128, 256], "int32"),
+    "mf": ("sbuf", [128, 256], "float32"), "mt": ("sbuf", [128, 256], "float32"), "ml": ("sbuf", [128, 256], "uint16"),
+    "ki": ("sbuf", [128, 256], "int32"), "ky": ("sbuf", [128, 256], "float32"), "k0": ("sbuf", [128, 256], "int32"),
+    "kf": ("sbuf", [128, 256], "float32"), "kz": ("sbuf", [128, 256], "int32"), "ab": ("sbuf", [128, 512], "int32"),
+    "khi": ("sbuf", [128, 512], "bfloat16"), "klo": ("sbuf", [128, 512], "bfloat16"), "kn": ("sbuf", [128, 512], "bfloat16"),
+    "eff_s": ("sbuf", [128, V], "bfloat16"), "pre_s": ("sbuf", [128, M], "bfloat16"),
+    "kp": ("sbuf", [128, M], "bfloat16"), "k3": ("sbuf", [128, 3 * M], "bfloat16"),
+    "p0": ("sbuf", [128, V], "float32"), "p1": ("sbuf", [128, V], "float32"),
+    "e": ("sbuf", [128, ECOL[8] + A], "bfloat16"), "stl": ("sbuf", [128, NE * A], "float16"),
+    "stb": ("sbuf", [128, V], "bfloat16"), "stf": ("sbuf", [128, V], "float32"),
+    "d0": ("sbuf", [128, NE * A], "float32"), "d1": ("sbuf", [128, NE * A], "float32"),
+    "c0": ("sbuf", [128, V], "bfloat16"), "c1": ("sbuf", [128, V], "bfloat16"),
+    "ng": ("sbuf", [128, V], "bfloat16"), "kg": ("sbuf", [128, V], "bfloat16"),
+    "w0": ("sbuf", [128, WIN], "bfloat16"), "w1": ("sbuf", [128, WIN], "bfloat16"),
+    "ones": ("sbuf", [128, 1024], "bfloat16"),
+    "rt0": ("sbuf", [128, 144], "uint16"), "rt1": ("sbuf", [128, 144], "uint16"), "rt2": ("sbuf", [128, 144], "uint16"),
+    "rf": ("sbuf", [128, 128], "float32"), "fin": ("sbuf", [128, 144], "float32"), "ysb": ("sbuf", [128, 256], "float32"),
+    "tot": ("sbuf", [128, 96], "float32"), "offs": ("sbuf", [128, 32], "float32"),
+    "ch": ("sbuf", [128, 128], "bfloat16"), "nb": ("sbuf", [128, 136], "bfloat16"), "tb": ("sbuf", [128, 136], "bfloat16"),
+    "il": ("sbuf", [128, 128], "uint16"), "sta": ("sbuf", [128, 64], "float32"), "of": ("sbuf", [128, 64], "float32"),
+    "ol": ("sbuf", [128, 64], "uint16"),
+    "e15": ("sbuf", [128, 160], "bfloat16"), "bp": ("sbuf", [128, 160], "bfloat16"), "bn": ("sbuf", [128, 160], "bfloat16"),
+    "ns": ("sbuf", [128, 160], "bfloat16"), "n1": ("sbuf", [128, 160], "bfloat16"), "ds": ("sbuf", [128, 160], "bfloat16"),
+    "cv": ("sbuf", [128, 7 * 160], "bfloat16"), "i2k": ("sbuf", [128, 128], "bfloat16"), "i32": ("sbuf", [128, 128], "float32"),
+    "sh": ("sbuf", [128, 128], "bfloat16"), "bg": ("sbuf", [128, 128], "bfloat16"), "bgn": ("sbuf", [128, 128], "bfloat16"),
+    "ta": ("sbuf", [128, 160], "bfloat16"), "tc": ("sbuf", [128, 160], "bfloat16"), "one32": ("sbuf", [128, 128], "float32"),
+    "mm": ("sbuf", [128, 6 * 128], "bfloat16"), "fc": ("sbuf", [128, 64], "float32"),
+    "ps_n": ("psum", [128, 512], "float32"), "ps_d": ("psum", [128, 512], "float32"),
+    "ps_v0": ("psum", [128, 512], "float32"), "ps_i0": ("psum", [128, 512], "float32"), "ps_s0": ("psum", [128, 512], "float32"),
+    "ps_v1": ("psum", [128, 512], "float32"), "ps_i1": ("psum", [128, 512], "float32"), "ps_s1": ("psum", [128, 512], "float32"),
+}
+SEMAPHORES = (["v", "s", "p", "q", "ls"] + ["dm%d" % i for i in range(16)]
+              + ["at%d" % i for i in range(RO)] + ["ag%d" % i for i in range(RO)])
+
+
+def engine_split(topo, src, dsts):
+    near = [d for d in dsts if d in topo.cores_of(src)]
+    far = [d for d in dsts if d not in near]
+    res = {}
+    used = set()
+    if far:
+        pool = topo.engines(src, far[0])
+        n = 1
+        while 2 * n * len(far) <= len(pool):
+            n *= 2
+        for i, d in enumerate(far):
+            res[d] = pool[i * n:(i + 1) * n]
+        used = set(pool)
+    for d in near:
+        pool = topo.engines(src, d)
+        rest = [x for x in pool if x not in used]
+        res[d] = rest[len(rest) - len(pool) // 2:]
+    return res
+
+
+def rank_program(g, core, T, topo):
+    r = T.rank_of(core)
+    if r is None:
+        return
+    cores = list(T.cores)
+    N = len(cores)
+    Q = {"v": g.vector, "s": g.scalar, "p": g.tensor, "q": g, "y": g.sync}
+    hist = {}
+    known = {k: {} for k in Q}
+    count = {}
+    ndma = [0]
+
+    def S(name, lo, hi, step=1, p=None):
+        ps = slice(None) if p is None else p
+        ap = T[name][ps, lo:hi:step] if step != 1 else T[name][ps, lo:hi]
+        if name.startswith("ps_"):
+            return (ap, name, 0, 512)
+        return (ap, name, lo, hi)
+
+    def span(x, lo, hi):
+        return x[:2] + (lo, hi)
+
+    def IND(win, lst):
+        return (win[0].indirect(lst[0]), win[1], win[2], win[3], lst)
+
+    def spans(xs):
+        return [x[1:4] for x in xs if isinstance(x, tuple)]
+
+    def lists(xs):
+        return [x[4][1:4] for x in xs if isinstance(x, tuple) and len(x) == 5]
+
+    def need(q, ev):
+        sem, n, snap = ev
+        if known[q].get(sem, 0) < n:
+            Q[q].wait_ge(T.sem[sem], n)
+            known[q][sem] = n
+            for k in snap:
+                if known[q].get(k, 0) < snap[k]:
+                    known[q][k] = snap[k]
+
+    def order(q, outs, ins, dma=False):
+        rd = spans(ins) + lists(ins) + lists(outs)
+        wr = spans(outs)
+        best = {}
+        for acc, w in [(a, False) for a in rd] + [(a, True) for a in wr]:
+            bank = acc[0].startswith("ps_")
+            for lo, hi, hw, ev, hq in hist.get(acc[0], []):
+                if lo < acc[2] and acc[1] < hi:
+                    same = hq == q and not dma
+                    if ((hw or w) and not (same and q == "p")) or (not same and bank):
+                        if ev[0] not in best or best[ev[0]][1] < ev[1]:
+                            best[ev[0]] = ev
+        for k in best:
+            need(q, best[k])
+        return rd, wr
+
+    def note(q, rd, wr, sem, n, seen):
+        count[sem] = count.get(sem, 0) + n
+        ev = (sem, count[sem], dict(seen))
+        for acc, w in [(a, False) for a in rd] + [(a, True) for a in wr]:
+            hist.setdefault(acc[0], []).append((acc[1], acc[2], w, ev, q))
+
+    def raw(x):
+        return x[0] if isinstance(x, tuple) else x
+
+    def op(q, call, outs, ins):
+        rd, wr = order(q, outs, ins)
+        call().then_inc(T.sem[q], 1)
+        note(q, rd, wr, q, 1, known[q])
+
+    def copy(o, i):
+        op("v", lambda: g.vector.tensor_copy(o[0], i[0]), [o], [i])
+
+    def tt(o, a, b, f):
+        op("v", lambda: g.vector.tensor_tensor(o[0], a[0], b[0], f), [o], [a, b])
+
+    def ts(o, a, s1, f0, s2=None, f1=None):
+        if f1 is None:
+            op("v", lambda: g.vector.tensor_scalar(o[0], a[0], raw(s1), None, f0), [o], [a, s1])
+        else:
+            op("v", lambda: g.vector.tensor_scalar(o[0], a[0], raw(s1), raw(s2), f0, f1), [o], [a, s1, s2])
+
+    def fill(o, c):
+        op("v", lambda: g.vector.memset(o[0], c), [o], [])
+
+    def scan(o, d, init):
+        one = S("ones", 0, o[3] - o[2])
+        op("v", lambda: g.vector.tensor_tensor_scan(o[0], one[0], d[0], raw(init), Op.mult, Op.add), [o], [one, d, init])
+
+    def act(o, i, f, bias=None, scale=None, acc=None):
+        kw = {}
+        if bias is not None:
+            kw["bias"] = raw(bias)
+        if scale is not None:
+            kw["scale"] = raw(scale)
+        if acc is not None:
+            kw["accum_out"] = acc[0]
+        op("s", lambda: g.scalar.activation(o[0], i[0], f, **kw), [o, acc], [i, bias, scale])
+
+    def mms(items):
+        rd, wr = order("p", [x[0] for x in items], [x[1] for x in items] + [x[2] for x in items])
+        last = None
+        for o, l, x, st, sp in items:
+            last = g.tensor.matmul(o[0], l[0], x[0], st, sp)
+        last.then_inc(T.sem.p, 1)
+        note("p", rd, wr, "p", 1, known["p"])
+
+    def iota(o, pat, base, cm):
+        op("q", lambda: g.iota(o[0], pat, base, cm, allow_small_or_imprecise_dtypes=True), [o], [])
+
+    def select(o, i, pat, f, base, cm):
+        op("q", lambda: g.affine_select(o[0], i[0], pat, f, 0.0, base, cm), [o], [i])
+
+    def band(o, i, t, pat, base, lo, hi):
+        select(t, i, pat, Op.is_ge, base - lo, -1)
+        select(o, t, [[-a, n] for a, n in pat], Op.is_ge, hi - base, 1)
+
+    def dmas(q, pairs):
+        sem = "dm%d" % ndma[0]
+        ndma[0] += 1
+        rd, wr = order(q, [x[0] for x in pairs], [x[1] for x in pairs], True)
+        for o, i in pairs:
+            Q[q].dma_start(raw(o), raw(i)).then_inc(T.sem[sem], 16)
+        note("dma", rd, wr, sem, 16 * len(pairs), known[q])
+
+    def send(src, dsts, dst, sem):
+        order("q", [], [src], True)
+        eng = engine_split(topo, core, dsts)
+        trs = []
+        for d in dsts:
+            rid, pid = topo.addr(d, core)
+            trs.append(RemoteDMATransfer(dst_ids=[DstId(rid=rid, pnc=pid)], dma_engine_mask=sum(1 << x for x in eng[d]),
+                                         remote_sem=T.sem[sem], src=src[0], dst=dst[0]))
+            count["ls"] = count.get("ls", 0) + len(eng[d])
+        g.remote_dma_fused(trs, local_sem=T.sem.ls)
+
+    def landing(regs, sem, n):
+        if n:
+            note("far", [], spans(regs), sem, n, {})
+
+    def tot_dsts(q, rnd):
+        if q == N - 1:
+            return [cores[k] for k in range(N - 1)] if rnd > 0 else []
+        return [cores[k] for k in range(q + 1, N)]
+
+    def tot(rnd, a, b):
+        return S("tot", 32 * rnd + a, 32 * rnd + b)
+
+    def tot_exchange(rnd):
+        if tot_dsts(r, rnd):
+            send(tot(rnd, 8 * r, 8 * r + 8), tot_dsts(r, rnd), tot(rnd, 8 * r, 8 * r + 8), "at%d" % rnd)
+        frm = [q for q in range(N) if core in tot_dsts(q, rnd)]
+        n = sum(len(engine_split(topo, cores[q], tot_dsts(q, rnd))[core]) for q in frm)
+        landing([tot(rnd, 8 * q, 8 * q + 8) for q in frm], "at%d" % rnd, n)
+
+    def go_exchange(nm, rnd):
+        send(S(nm, 128, 144), [cores[(r + 1) % N]], S(nm, 0, 16), "ag%d" % rnd)
+        landing([S(nm, 0, 16)], "ag%d" % rnd, len(engine_split(topo, cores[(r - 1) % N], [core])[core]))
+
+    eff, pre, kp = S("eff_s", 0, V), S("pre_s", 0, M), S("kp", 0, M)
+
+    def effects(a, b, lst, acc):
+        act(S("e", ECOL[a], ECOL[a] + A * (b - a)), IND(eff, lst), Fn.Identity, acc=acc)
+
+    dmas("y", [(S("ki", 0, 256), T.kid[:])])
+    dmas("s", [(S("todo_s", 0, 128), T.todo[:])])
+    dmas("s", [(eff, T.eff[:])])
+    dmas("y", [(S("mi", 32 * b + 16 * h, 32 * b + 16 * h + 16), T.meth[h:8:2, 512 * b:512 * b + 512])
+               for b in range(4) for h in range(2)])
+    dmas("y", [(pre, T.pre[:])])
+    fill(S("ones", 0, 1024), 1.0)
+    fill(kp, 0.0)
+    fill(S("e", ECOL[0] - 1, ECOL[1], ECOL[1] - ECOL[0]), 0.0)
+    fill(S("e", ECOL[5] - 1, ECOL[5]), 0.0)
+    for k in range(RO):
+        fill(tot(k, 8 * r, 8 * r + 8), 0.0)
+    lin = [[1, 160]]
+    o160, ta, tc = S("ones", 0, 160), S("ta", 0, 160), S("tc", 0, 160)
+    ta8, tc8 = S("ta", 0, 128), S("tc", 0, 128)
+    select(S("e15", 0, 160), o160, [[0, 10], [1, 16]], Op.is_equal, -15, 0)
+    band(S("bp", 0, 160), S("e15", 0, 160), ta, lin, 0, 0, 15)
+    band(S("bg", 0, 128), S("ones", 0, 128), tc8, [[16, 8], [0, 16]], 15, 0, 15)
+    for w, a, b in (("w1", 0, 1024), ("w1", 1024, V), ("w1", V, V + PAD), ("w0", 0, 1024), ("w0", 1024, PAD + LOW)):
+        act(S(w, a, b), S("ones", 0, b - a), Fn.Copy, scale=0.0)
+    act(S("bn", 0, 160), S("bp", 0, 160), Fn.Copy, scale=-1.0)
+    act(S("bgn", 0, 128), S("bg", 0, 128), Fn.Copy, scale=-8192.0)
+    band(S("ns", 0, 160), S("e15", 0, 160), ta, lin, 0, 6, 7)
+    band(S("n1", 0, 160), S("e15", 0, 160), tc, lin, 0, 4, 5)
+    copy(S("rt0", 0, 128), S("todo_s", 0, 128))
+    for a, b in ((0, 1), (1, 5), (5, 8)):
+        effects(a, b, S("rt0", 16 * a, 16 * b), tot(0, 8 * r + a, 8 * r + a + 1))
+    tot_exchange(0)
+    ts(S("k0", 0, 256), S("ki", 0, 256), 4095, Op.bitwise_and)
+    ts(S("ky", 0, 256), S("ki", 0, 256), -1.0, Op.mult, float(EMPTY + 4096 * EMPTY), Op.add)
+    ts(S("kf", 0, 256), S("k0", 0, 256), float(EMPTY), Op.not_equal, 1.0 / 4096, Op.max)
+    tt(S("kz", 0, 256), S("ky", 0, 256), S("kf", 0, 256), Op.mult)
+    ts(S("ab", 0, 256), S("kz", 0, 256), 4095, Op.bitwise_and)
+    ts(S("ab", 256, 512), S("kz", 0, 256), 12, Op.arith_shift_right)
+    copy(S("khi", 0, 512), S("ab", 0, 512))
+    ts(S("kn", 0, 512), S("ab", 0, 512), 0.0, Op.is_gt)
+    dmas("y", [(S("kp", 0, M, p=slice(v, 128, 16)), S(nm, c, c + 256))
+               for v, nm, c in [(0, "khi", 0), (2, "khi", 256), (8, "kn", 0), (9, "kn", 256)]])
+    tt(S("klo", 0, 512), S("ab", 0, 512), S("khi", 0, 512), Op.subtract)
+    dmas("y", [(span(S("kp", 0, M, p=slice(v, 128, 16)), M, M + 1), S("klo", c, c + 256)) for v, c in [(1, 0), (3, 256)]])
+    kp = span(kp, 0, M + 1)
+    ts(S("m2", 0, 128), S("mi", 0, 128), 4095, Op.bitwise_and)
+    ts(S("m2", 128, 256), S("mi", 0, 128), 12, Op.arith_shift_right)
+    copy(S("mf", 0, 256), S("m2", 0, 256))
+    op("v", lambda: g.vector.transpose(T.mt[:, 0:256], T.mf[:, 0:256]), [S("mt", 0, 256)], [S("mf", 0, 256)])
+    copy(S("ml", 0, 256), S("mt", 0, 256))
+    act(S("k3", 2 * M + V, 3 * M), S("w1", 0, V), Fn.Copy)
+    act(S("p0", 0, V), IND(pre, S("ml", 0, 128)), Fn.Identity, bias=-0.25)
+    dmas("y", [(S("k3", M + V * k, M + V * k + V), S("w1", 0, V)) for k in range(2)])
+    fill(S("k3", 2 * M, 2 * M + V), 0.0)
+    fill(S("nb", 0, 2), 0.0)
+    fill(S("tb", 0, 2), 0.0)
+    ts(S("stl", 0, NE * A, A), S("ones", 0, NE), 0.0, Op.mult)
+    copy(S("rf", 0, 128), S("todo_s", 0, 128))
+    tt(S("ds", 0, 160), S("n1", 0, 160), S("ns", 0, 160), Op.subtract)
+    ts(S("p1", 0, P1V), IND(pre, S("ml", 128, 128 + P1V // 16)), -0.25, Op.add)
+    ptab = [S("p0", 0, V), S("p1", 0, V)]
+    cn = ["c0", "c1"]
+
+    def kid_tables():
+        act(S("k3", 0, V), IND(kp, S("ml", 0, 128)), Fn.Identity)
+        copy(S("k3", V, M), IND(kp, S("ml", 128, 256)))
+        dmas("y", [(span(S("k3", 0, V, p=slice(10 + v, 128, 16)), 3 * M, 3 * M + 1), span(S("k3", V, M, p=slice(8 + v, 128, 16)), 0, M))
+                   for v in range(2)])
+        dmas("y", [(S("k3", M * k, M * k + M, p=slice(2 * k + v, 128, 16)), S("k3", 0, M, p=slice(v, 128, 16)))
+                   for k in (1, 2) for v in range(4)])
+        act(S("p1", P1V, V), IND(pre, S("ml", 128 + P1V // 16, 256)), Fn.Identity, bias=-0.25)
+
+    def constants():
+        pat = [[16, 8], [2, 16]]
+        iota(S("one32", 0, 128), [[0, 128]], 1, 0)
+        select(S("i32", 0, 128), S("one32", 0, 128), [[1, 128]], Op.is_equal, 0, -1)
+        iota(S("fc", 0, 64), [[16, 64]], 4096, 1)
+        iota(ta8, [[0, 64], [4096, 2]], 0, 0)
+        select(S("sh", 0, 128), ta8, [[1, 128]], Op.is_equal, -1, -1)
+        iota(tc8, [[0, 128]], 2048, 0)
+        select(S("i2k", 0, 128), tc8, [[1, 128]], Op.is_equal, 0, -1)
+        for a in range(2):
+            select(S("mm", 128 * a, 128 * a + 128), S("bg", 0, 128), [[-16, 8], [-2, 16]], Op.is_ge, 16 * a, 1)
+            select(S("mm", 256 + 128 * a, 384 + 128 * a), S("bg", 0, 128), pat, Op.is_gt, -16 * a, -1)
+            band(S("mm", 512 + 128 * a, 640 + 128 * a), S("bgn", 0, 128), (ta8, tc8)[a], pat, -16 * a, -1, 0)
+        select(ta, o160, [[0, 10], [-1, 16]], Op.is_ge, 3, 0)
+        band(S("cv", 0, 160), ta, tc, [[16, 10], [2, 16]], -16, -1, 0)
+        for j in range(3):
+            select(S("cv", 160 * j + 160, 160 * j + 320), S("cv", 0, 160), [[0, 10], [-1, 16]], Op.is_ge, j, 0)
+            select(S("cv", 160 * j + 640, 160 * j + 800), S("cv", 0, 160), [[0, 10], [1, 16]], Op.is_ge, -j - 1, 0)
+
+    for rnd in range(RO):
+        rt, last = "rt%d" % rnd, rnd == RO - 1
+        stn = "stf" if last else "stb"
+
+        def lst(a, b):
+            return S(rt, 16 * a, 16 * b)
+
+        def direct(k, a, b):
+            tt(S(cn[k], A * a, A * b), IND(ptab[k], lst(a, b)), S(stn, A * a, A * b), Op.is_le)
+
+        def states(a, b, init):
+            scan(S(stn, A * a, A * b), S("e", ECOL[a] - 1, ECOL[a] - 1 + A * (b - a)), init)
+
+        def count_rows(a, b):
+            act(S("ng", A * a, A * b), IND(span(S("k3", 0, V), 3 * M, 3 * M + 1), lst(a, b)), Fn.Identity)
+
+        def rows_to_list(ps, sel, src, h, start, stop):
+            a, b = PARTS[h]
+            mms([(S(ps, a, b), S(sel, 15 - k, 143 - k), S(src, 16 * a + k, 16 * b, 16), start and k == 0, stop and k == 15)
+                 for k in range(16)])
+
+        def counts(h):
+            rows_to_list("ps_n", "ns", "ng", h, True, True)
+            rows_to_list("ps_d", "ds", "ng", h, True, True)
+
+        def votes(k, h):
+            rows_to_list("ps_v%d" % h, ("bn", "bp")[k], cn[k], h, k == 0, k == 1)
+
+        def heads(h):
+            a, b = PARTS[h]
+            mms([(S("ps_i%d" % h, a, b), S("i32", 0, 128), S("rf", a, b), True, False),
+                 (S("ps_s%d" % h, 64 + a // 2, 64 + b // 2), S("i32", 0, 128), S("fc", a // 2, b // 2), True, False)])
+
+        def first_counts(h):
+            a, b = PARTS[h]
+            act(S("nb", 2 + a, 2 + b), S("ps_n", a, b), Fn.Identity)
+            mms([(S("ps_i%d" % h, a, b), S("sh", 0, 128), S("nb", 2 + a, 2 + b), False, False)]
+                + [(S("ps_s%d" % h, 64 + a // 2, 64 + b // 2), S("mm", 512 + 128 * j, 640 + 128 * j), S("nb", 2 + a + j, 2 + b + j, 2), False, False)
+                   for j in range(2)])
+
+        def choose(h):
+            a, b = PARTS[h]
+            pi, ps = "ps_i%d" % h, "ps_s%d" % h
+            ts(S("ch", a, b), S("ps_v%d" % h, a, b), 0.0, Op.is_gt)
+            mms([(S(pi, a, b), S("i2k", 0, 128), S("ch", a, b), False, False)])
+            tt(S("tb", 2 + a, 2 + b), S("ch", a, b), S("ps_d", a, b), Op.mult)
+            mms([(S(pi, a, b), S("sh", 0, 128), S("tb", 2 + a, 2 + b), False, True)])
+            mms([(S(ps, 64 + a // 2, 64 + b // 2), S("mm", 512 + 128 * j, 640 + 128 * j), S("tb", 2 + a + j, 2 + b, 2), False, j == 1)
+                 for j in range(2)]
+                + [(S(ps, a // 2, b // 2), S("mm", 128 * j, 128 * j + 128), S(nm, a + j, b + j - 1, 2), nm == "nb" and j == 0, nm == "tb" and j == 3)
+                   for nm in ("nb", "tb") for j in range(4)])
+
+        def kid_list(h):
+            a, b = PARTS[h]
+            copy(S("il", a, b), S("ps_i%d" % h, a, b))
+
+        def starts(h):
+            a, b = PARTS[h][0] // 2, PARTS[h][1] // 2
+            scan(S("sta", a, b), S("ps_s%d" % h, a, b), S("sta", a - 1, a) if a else 0.0)
+            tt(S("of", a, b), S("sta", a, b), S("ps_s%d" % h, 64 + a, 64 + b), Op.max)
+            copy(S("ol", a, b), S("of", a, b))
+
+        def kids(j):
+            act(S("kg", 512 * j, 512 * j + 512), IND(span(S("k3", 0, 3 * M), 0, 3 * M + 1), S("il", 32 * j, 32 * j + 32)), Fn.Identity)
+
+        def place(j):
+            tt(IND(S("w1" if j else "w0", PAD, WIN), S("ol", 16 * j, 16 * j + 16)), S("kg", 512 * j, 512 * j + 512, 2),
+               S("kg", 512 * j + 1, 512 * j + 512, 2), Op.add)
+
+        def row_list(ps, w, a, start, stop):
+            o = S(ps, a, a + 64)
+            items = []
+            for k in range(16):
+                j = 0 if k < 13 else 16 - k
+                items.append((o, S("cv", 160 * j + 16 - k, 160 * j + 144 - k), S(w, PAD + 16 * a + k, PAD + 16 * a + 1024, 16), start and k == 0, False))
+            for k in (13, 14, 15):
+                j = 19 - k
+                items.append((o, S("cv", 160 * j + 32 - k, 160 * j + 160 - k), S(w, 16 * a + k, 16 * a + 1024, 16), False, stop and k == 15))
+            mms(items)
+
+        if rnd == 0:
+            constants()
+            scan(S("offs", 0, 8 * r + 5), tot(0, 0, 8 * r + 5), 0.0)
+            states(0, 1, S("offs", 8 * r - 1, 8 * r) if r else 0.0)
+            states(1, 5, S("offs", 8 * r, 8 * r + 1))
+            states(5, 8, S("offs", 8 * r + 4, 8 * r + 5))
+            kid_tables()
+            heads(0)
+            heads(1)
+            direct(0, 0, 4)
+            votes(0, 0)
+            direct(0, 4, 8)
+            votes(0, 1)
+            count_rows(0, 4)
+            counts(0)
+            count_rows(4, 6)
+            direct(1, 0, 4)
+            first_counts(0)
+            count_rows(6, 8)
+            votes(1, 0)
+            direct(1, 4, 6)
+            choose(0)
+            counts(1)
+            kid_list(0)
+            first_counts(1)
+            kids(1)
+            direct(1, 6, 8)
+            starts(0)
+        else:
+            def off(s):
+                if s == 0:
+                    return S("offs", 8 * r - 2, 8 * r - 1) if r else 0.0
+                return S("offs", 8 * r - 2 + s, 8 * r - 1 + s) if (r or s > 1) else tot(rnd, 31, 32)
+
+            def local(s):
+                scan(S("stl", A * (s - 1) + 1, A * s), S("e", ECOL[s], ECOL[s] + A - 1), 0.0)
+
+            def diff(k, a, b):
+                tt(S(("d0", "d1")[k], A * (a - 1), A * (b - 1)), IND(ptab[k], lst(a, b)), S("stl", A * (a - 1), A * (b - 1)), Op.subtract)
+
+            def sign(k, s):
+                act(S(cn[k], A * s, A * s + A), S(("d0", "d1")[k], A * (s - 1), A * s), Fn.Sign, bias=off(s), scale=-1.0)
+
+            for s in range(1, 5):
+                effects(s, s + 1, lst(s, s + 1), tot(rnd, 8 * r + s - 1, 8 * r + s))
+            e56, t56 = S("e", ECOL[5], ECOL[7]), tot(rnd, 8 * r + 4, 8 * r + 5)
+            op("v", lambda: g.vector.tensor_reduce(t56[0], e56[0], Ax.X, Op.add), [t56], [e56])
+            tot_exchange(rnd)
+            iota(S("w1", 0, PAD + V), [[0, PAD + V]], 0, 0)
+            iota(S("w0", 0, PAD + LOW), [[0, PAD + LOW]], 0, 0)
+            local(1)
+            diff(0, 1, 2)
+            local(2)
+            diff(1, 1, 3)
+            effects(0, 1, lst(0, 1), None)
+            count_rows(0, 4)
+            count_rows(4, 8)
+            local(3)
+            local(4)
+            diff(0, 2, 5)
+            copy(S("rf", 0, 128), S(rt, 0, 128))
+            heads(0)
+            heads(1)
+            counts(0)
+            diff(1, 3, 5)
+            scan(S("offs", 0, 8 * r + 4), tot(rnd, 0, 8 * r + 4), tot(rnd, 31, 32))
+            states(0, 1, off(0))
+            states(5, 8, off(5))
+            direct(0, 0, 1)
+            direct(1, 0, 1)
+            first_counts(0)
+            counts(1)
+            for k in range(2):
+                for s in range(1, 4):
+                    sign(k, s)
+                votes(k, 0)
+            first_counts(1)
+            direct(0, 5, 8)
+            sign(0, 4)
+            sign(1, 4)
+            direct(1, 5, 6)
+            choose(0)
+            votes(0, 1)
+            kid_list(0)
+            kids(1)
+            direct(1, 6, 8)
+            starts(0)
+        votes(1, 1)
+        kids(0)
+        choose(1)
+        kid_list(1)
+        kids(2)
+        kids(3)
+        place(1)
+        starts(1)
+        place(2)
+        place(3)
+        row_list("ps_n", "w1", 64, True, True)
+        row_list("ps_d", "w1", 0, True, False)
+        place(0)
+        row_list("ps_d", "w0", 0, False, True)
+        if not last:
+            nxt = "rt%d" % (rnd + 1)
+            ts(S(nxt, 80, 144), S("ps_n", 64, 128), -1.0, Op.mult, float(EMPTY), Op.add)
+            go_exchange(nxt, rnd)
+            effects(7, 8, S(nxt, 112, 128), tot(rnd + 1, 8 * r + 6, 8 * r + 7))
+            effects(8, 9, S(nxt, 128, 144), tot(rnd + 1, 8 * r + 7, 8 * r + 8))
+            copy(S("e", ECOL[5], ECOL[7]), IND(eff, S(nxt, 80, 112)))
+            ts(S(nxt, 16, 80), S("ps_d", 0, 64), -1.0, Op.mult, float(EMPTY), Op.add)
+        else:
+            act(S("ysb", 0, 32), S("stf", 0, A, 8), Fn.Identity)
+            act(S("ysb", 160, 256), S("stf", 5 * A, V, 8), Fn.Identity)
+            act(S("fin", 80, 144), S("ps_n", 64, 128), Fn.Identity, bias=float(EMPTY), scale=-1.0)
+            go_exchange("fin", rnd)
+            for s in range(1, 5):
+                ts(S("ysb", 32 * s, 32 * s + 32), S("stl", A * (s - 1), A * s, 8), off(s), Op.add)
+            dmas("s", [(T.ys[:], S("ysb", 0, 256))])
+            ts(S("fin", 16, 80), S("ps_d", 0, 64), -1.0, Op.mult, float(EMPTY), Op.add)
+            dmas("y", [(T.yp[:, 16:128], S("fin", 16, 128))])
+            dmas("y", [(T.yp[:, 0:16], S("fin", 0, 16))])
+    for sem in count:
+        g.wait_ge(T.sem[sem], count[sem])

@@ -1,53 +1,70 @@
 from concourse.bass import DstId, RemoteDMATransfer
-from concourse.mybir import AluOpType as Op, ActivationFunctionType as Fn, AxisListType as Ax
+from concourse.mybir import AluOpType as Op, ActivationFunctionType as Fn
 
-V, A, M, RO = 2048, 256, 4096, 3
+V, A, M, RO, N = 2048, 256, 4096, 3, 4
+B = 128 // N
 EMPTY = V - 1
-NE = 4
 PAD = 16
-WIN = PAD + 5248
-LOW = 1024
-P1V = 640
-ECOL = [16, 288, 544, 800, 1056, 1328, 1584, 1840, 2096]
+SPARE = 1152
+W0 = SPARE + PAD
+LOW = 1021
 PARTS = [(0, 64), (64, 128)]
+NEAR = 5
+FAR = [(0, 6, 8, "ps_v0"), (1, 6, 8, "ps_s"), (0, 5, 6, "ps_i0"), (1, 5, 6, "ps_i1")]
+
+START = """todo out, meth, kid, pre, eff, todo own, one32:0, k3:4096, k3:4608, zero:0, e:0, ct:0, ct:264, iw:0, nb:0, tb:0, ones:0,
+    w:1152, w:1664, w:2176, w:2688, w:3200, at, gaps,
+    m2:0, m2:32, mf:32, mf:0, mf:96, k0:0, ky:0, kf:0, kz:0, methods, ab:128, ab:0, khi:0, khi rows, ml:0, klo:0, klo rows,
+    cn:768, cn:0, p0 table, p1 table, todo in, ih:0,
+    lm:0, ip:0, im:0, fc:0, e15:0, ta:160, ta:0, bg:0, bp:0, i2k:0, ta:320, mm:128, sh:0, mm:0, mm:256, mm:384,
+    nd:0, nd:16, nd:8, zero rows, kt:0, kt:1024, fh:0, bn:0, bgn:0,
+    ta:480, ta:640, mm:512, mm:640, ta:800, ta:960, cv:0, cv:960, cv:320, cv:800, cv:160, cv:640, cv:480,
+    rt:0, count rows, kid table, kid rows"""
+ROUND = """rt:80, arr:0, cond:1536, e:1296, rotate, w:1152, rt:16, rt:0, cond:3328, e:16, sum0, cond:3584, minus16, minus15,
+    cond:1280, ng:1536, ng:1024, sum1, rf:0, stb:0, ng:0, counts1, minus05, minus06, c0:1024, plus06, c0:0, plus05, plus15,
+    c0:1536, c0:1280, plus16, eights, counts0, c1:1024, c1:1536, votes01, c1:0, c1:1280, votes00, ct:272, ct:8, votes11,
+    turn1, turn0, ch:64, votes10, nb:2, tb:66, ysb:0, nb:66, heads, ys out, ys own, ay, ys in, first0, ch:0, first1, index1,
+    steps nb, tb:2, il:64, steps tb, kg:1024, index0, sta:0, of:0, il:0, ol:0, kg:1536, w:32, kg:512, w:48, kg:0, w:16,
+    zero:256, zero:768, zero:1280, zero:1792, row64, w:0, arr:16, fin:80, row0, rotate out, fin:0, fin:16,
+    yp out, yp own, ap, yp in"""
 
 SCRATCH = {
-    "todo_s": ("sbuf", [128, 128], "int32"), "mi": ("sbuf", [128, 128], "int32"), "m2": ("sbuf", [128, 256], "int32"),
-    "mf": ("sbuf", [128, 256], "float32"), "mt": ("sbuf", [128, 256], "float32"), "ml": ("sbuf", [128, 256], "uint16"),
-    "ki": ("sbuf", [128, 256], "int32"), "ky": ("sbuf", [128, 256], "float32"), "k0": ("sbuf", [128, 256], "int32"),
-    "kf": ("sbuf", [128, 256], "float32"), "kz": ("sbuf", [128, 256], "int32"), "ab": ("sbuf", [128, 512], "int32"),
-    "khi": ("sbuf", [128, 512], "bfloat16"), "klo": ("sbuf", [128, 512], "bfloat16"), "kn": ("sbuf", [128, 512], "bfloat16"),
-    "eff_s": ("sbuf", [128, V], "bfloat16"), "pre_s": ("sbuf", [128, M], "bfloat16"),
-    "kp": ("sbuf", [128, M], "bfloat16"), "k3": ("sbuf", [128, 3 * M], "bfloat16"),
-    "p0": ("sbuf", [128, V], "float32"), "p1": ("sbuf", [128, V], "float32"),
-    "e": ("sbuf", [128, ECOL[8] + A], "bfloat16"), "stl": ("sbuf", [128, NE * A], "float16"),
-    "stb": ("sbuf", [128, V], "bfloat16"), "stf": ("sbuf", [128, V], "float32"),
-    "d0": ("sbuf", [128, NE * A], "float32"), "d1": ("sbuf", [128, NE * A], "float32"),
+    "todo_s": ("sbuf", [128, 128], "int32"), "mi": ("sbuf", [128, 32], "int32"), "m2": ("sbuf", [128, 64], "int32"),
+    "mf": ("sbuf", [128, 128], "float32"), "ml": ("sbuf", [128, 128], "uint16"),
+    "ki": ("sbuf", [128, 128], "int32"), "ky": ("sbuf", [128, 128], "float32"), "k0": ("sbuf", [128, 128], "int32"),
+    "kf": ("sbuf", [128, 128], "float32"), "kz": ("sbuf", [128, 128], "int32"), "ab": ("sbuf", [128, 256], "int32"),
+    "khi": ("sbuf", [128, 256], "bfloat16"), "klo": ("sbuf", [128, 256], "bfloat16"),
+    "eff_s": ("sbuf", [128, V], "bfloat16"), "k3": ("sbuf", [128, 3 * M], "bfloat16"),
+    "p0": ("sbuf", [128, V], "bfloat16"), "p1": ("sbuf", [128, V], "bfloat16"),
+    "cn": ("sbuf", [128, V], "bfloat16"), "kt": ("sbuf", [128, V], "bfloat16"),
+    "e": ("sbuf", [128, PAD + V], "bfloat16"), "stb": ("sbuf", [128, V], "bfloat16"), "cond": ("sbuf", [128, 2 * V], "bfloat16"),
     "c0": ("sbuf", [128, V], "bfloat16"), "c1": ("sbuf", [128, V], "bfloat16"),
     "ng": ("sbuf", [128, V], "bfloat16"), "kg": ("sbuf", [128, V], "bfloat16"),
-    "w0": ("sbuf", [128, WIN], "bfloat16"), "w1": ("sbuf", [128, WIN], "bfloat16"),
-    "ones": ("sbuf", [128, 1024], "bfloat16"),
-    "rt0": ("sbuf", [128, 144], "uint16"), "rt1": ("sbuf", [128, 144], "uint16"), "rt2": ("sbuf", [128, 144], "uint16"),
-    "rf": ("sbuf", [128, 128], "float32"), "fin": ("sbuf", [128, 144], "float32"), "ysb": ("sbuf", [128, 256], "float32"),
-    "tot": ("sbuf", [128, 96], "float32"), "offs": ("sbuf", [128, 32], "float32"),
+    "w": ("sbuf", [128, W0 + M], "bfloat16"), "zero": ("sbuf", [128, V], "bfloat16"), "ones": ("sbuf", [128, 160], "bfloat16"),
+    "rt0": ("sbuf", [128, 128], "uint16"), "rt1": ("sbuf", [128, 128], "uint16"), "rt2": ("sbuf", [128, 128], "uint16"),
+    "rf": ("sbuf", [128, 128], "float16"), "fin": ("sbuf", [128, 128], "float32"), "ysb": ("sbuf", [128, 256], "float32"),
+    "tot": ("sbuf", [128, 2], "float32"), "arr": ("sbuf", [128, 32], "float32"), "ct": ("sbuf", [128, 2 * 264], "bfloat16"),
     "ch": ("sbuf", [128, 128], "bfloat16"), "nb": ("sbuf", [128, 136], "bfloat16"), "tb": ("sbuf", [128, 136], "bfloat16"),
     "il": ("sbuf", [128, 128], "uint16"), "sta": ("sbuf", [128, 64], "float32"), "of": ("sbuf", [128, 64], "float32"),
     "ol": ("sbuf", [128, 64], "uint16"),
+    "tst": ("dram", [N, 128, 32], "int32"), "tld": ("dram", [N, 128, 32], "int32"),
+    "yst": ("dram", [N, 128, 64], "float32"), "yld": ("dram", [N, 128, 64], "float32"),
+    "pst": ("dram", [N, 128, 32], "float32"), "pld": ("dram", [N, 128, 32], "float32"),
     "e15": ("sbuf", [128, 160], "bfloat16"), "bp": ("sbuf", [128, 160], "bfloat16"), "bn": ("sbuf", [128, 160], "bfloat16"),
-    "ns": ("sbuf", [128, 160], "bfloat16"), "n1": ("sbuf", [128, 160], "bfloat16"), "ds": ("sbuf", [128, 160], "bfloat16"),
-    "cv": ("sbuf", [128, 7 * 160], "bfloat16"), "i2k": ("sbuf", [128, 128], "bfloat16"), "i32": ("sbuf", [128, 128], "float32"),
+    "nd": ("sbuf", [128, 24], "bfloat16"), "cv": ("sbuf", [128, 7 * 160], "bfloat16"), "i2k": ("sbuf", [128, 128], "bfloat16"),
+    "ip": ("sbuf", [128, 128], "bfloat16"), "im": ("sbuf", [128, 128], "bfloat16"), "ih": ("sbuf", [128, 128], "float16"),
     "sh": ("sbuf", [128, 128], "bfloat16"), "bg": ("sbuf", [128, 128], "bfloat16"), "bgn": ("sbuf", [128, 128], "bfloat16"),
-    "ta": ("sbuf", [128, 160], "bfloat16"), "tc": ("sbuf", [128, 160], "bfloat16"), "one32": ("sbuf", [128, 128], "float32"),
-    "mm": ("sbuf", [128, 6 * 128], "bfloat16"), "fc": ("sbuf", [128, 64], "float32"),
-    "ps_n": ("psum", [128, 512], "float32"), "ps_d": ("psum", [128, 512], "float32"),
-    "ps_v0": ("psum", [128, 512], "float32"), "ps_i0": ("psum", [128, 512], "float32"), "ps_s0": ("psum", [128, 512], "float32"),
-    "ps_v1": ("psum", [128, 512], "float32"), "ps_i1": ("psum", [128, 512], "float32"), "ps_s1": ("psum", [128, 512], "float32"),
+    "ta": ("sbuf", [128, 7 * 160], "bfloat16"), "one32": ("sbuf", [128, 512], "float32"),
+    "mm": ("sbuf", [128, 6 * 128], "bfloat16"), "fc": ("sbuf", [128, 128], "float32"), "fh": ("sbuf", [128, 128], "float16"),
+    "iw": ("sbuf", [128, 256], "float32"), "lm": ("sbuf", [128, 128], "float32"),
+    "ps_c0": ("psum", [128, 512], "float32"), "ps_c1": ("psum", [128, 512], "float32"),
+    "ps_v0": ("psum", [128, 512], "float32"), "ps_i0": ("psum", [128, 512], "float32"), "ps_s": ("psum", [128, 512], "float32"),
+    "ps_v1": ("psum", [128, 512], "float32"), "ps_i1": ("psum", [128, 512], "float32"), "ps_o": ("psum", [128, 512], "float32"),
 }
-SEMAPHORES = (["v", "s", "p", "q", "ls"] + ["dm%d" % i for i in range(16)]
-              + ["at%d" % i for i in range(RO)] + ["ag%d" % i for i in range(RO)])
+SEMAPHORES = ["v", "s", "p", "q", "ls", "at", "ay", "ap"] + ["dm%d" % i for i in range(24)]
 
 
-def engine_split(topo, src, dsts):
+def engine_split(topo, src, dsts, most):
     near = [d for d in dsts if d in topo.cores_of(src)]
     far = [d for d in dsts if d not in near]
     res = {}
@@ -64,7 +81,7 @@ def engine_split(topo, src, dsts):
         pool = topo.engines(src, d)
         rest = [x for x in pool if x not in used]
         res[d] = rest[len(rest) - len(pool) // 2:]
-    return res
+    return {d: res[d][::max(1, len(res[d]) // most)] for d in res}
 
 
 def rank_program(g, core, T, topo):
@@ -72,31 +89,62 @@ def rank_program(g, core, T, topo):
     if r is None:
         return
     cores = list(T.cores)
-    N = len(cores)
+    others = [q for q in range(N) if q != r]
     Q = {"v": g.vector, "s": g.scalar, "p": g.tensor, "q": g, "y": g.sync}
     hist = {}
     known = {k: {} for k in Q}
     count = {}
     ndma = [0]
+    ALL = (1 << 128) - 1
 
     def S(name, lo, hi, step=1, p=None):
         ps = slice(None) if p is None else p
         ap = T[name][ps, lo:hi:step] if step != 1 else T[name][ps, lo:hi]
-        if name.startswith("ps_"):
-            return (ap, name, 0, 512)
-        return (ap, name, lo, hi)
+        rows = ALL if p is None else sum(1 << x for x in range(128)[p])
+        return (ap, (name, 0, 512, ALL) if name.startswith("ps_") else (name, lo, hi, rows), None)
 
-    def span(x, lo, hi):
-        return x[:2] + (lo, hi)
+    def D(name, lo, hi=None):
+        return (T[name][lo], (name, lo, lo + 1, ALL), None) if hi is None else (T[name][lo:hi], (name, lo, hi, ALL), None)
+
+    def blk(s):
+        return slice(B * s, B * s + B)
+
+    def row(v, lo=0, hi=128):
+        return slice(lo + v, hi, 16)
 
     def IND(win, lst):
-        return (win[0].indirect(lst[0]), win[1], win[2], win[3], lst)
+        return (win[0].indirect(lst[0]), win[1], lst)
 
     def spans(xs):
-        return [x[1:4] for x in xs if isinstance(x, tuple)]
+        return [x[1] for x in xs if isinstance(x, tuple)]
 
     def lists(xs):
-        return [x[4][1:4] for x in xs if isinstance(x, tuple) and len(x) == 5]
+        return [x[2][1] for x in xs if isinstance(x, tuple) and x[2]]
+
+    def meet(a, b):
+        return a[1] < b[2] and b[1] < a[2] and a[3] & b[3]
+
+    calls = []
+    phase = [0]
+
+    def later(name, outs, ins, issue):
+        calls.append((spans(ins) + lists(ins) + lists(outs), spans(outs), issue, phase[0], name))
+
+    def issue_all():
+        pre, seen = [], {}
+        for i, c in enumerate(calls):
+            acc = [(a, False) for a in c[0]] + [(a, True) for a in c[1]]
+            pre.append(set(j for a, w in acc for b, hw, j in seen.get(a[0], []) if (hw or w) and meet(a, b)))
+            for a, w in acc:
+                seen.setdefault(a[0], []).append((a, w, i))
+        names = [[x.strip() for x in s.split(",")] for s in (START + "," + ROUND, ROUND)]
+        left = sorted(range(len(calls)), key=lambda i: (calls[i][3], names[min(calls[i][3], 1)].index(calls[i][4]), i))
+        done = set()
+        while left:
+            i = next(i for i in left if pre[i] <= done)
+            left.remove(i)
+            done.add(i)
+            calls[i][2]()
 
     def need(q, ev):
         sem, n, snap = ev
@@ -113,10 +161,10 @@ def rank_program(g, core, T, topo):
         best = {}
         for acc, w in [(a, False) for a in rd] + [(a, True) for a in wr]:
             bank = acc[0].startswith("ps_")
-            for lo, hi, hw, ev, hq in hist.get(acc[0], []):
-                if lo < acc[2] and acc[1] < hi:
+            for b, hw, ev, hq in hist.get(acc[0], []):
+                if meet(acc, b):
                     same = hq == q and not dma
-                    if ((hw or w) and not (same and q == "p")) or (not same and bank):
+                    if ((hw or w) and q != "p" if same else hw or w or bank):
                         if ev[0] not in best or best[ev[0]][1] < ev[1]:
                             best[ev[0]] = ev
         for k in best:
@@ -127,15 +175,18 @@ def rank_program(g, core, T, topo):
         count[sem] = count.get(sem, 0) + n
         ev = (sem, count[sem], dict(seen))
         for acc, w in [(a, False) for a in rd] + [(a, True) for a in wr]:
-            hist.setdefault(acc[0], []).append((acc[1], acc[2], w, ev, q))
+            hist.setdefault(acc[0], []).append((acc, w, ev, q))
 
     def raw(x):
         return x[0] if isinstance(x, tuple) else x
 
     def op(q, call, outs, ins):
-        rd, wr = order(q, outs, ins)
-        call().then_inc(T.sem[q], 1)
-        note(q, rd, wr, q, 1, known[q])
+        def issue():
+            rd, wr = order(q, outs, ins)
+            call().then_inc(T.sem[q], 1)
+            note(q, rd, wr, q, 1, known[q])
+        o = outs[0][2][1] if outs[0][2] else outs[0][1]
+        later("%s:%d" % ("rt" if outs[0][1][0][:2] == "rt" else outs[0][1][0], o[1]), outs, ins, issue)
 
     def copy(o, i):
         op("v", lambda: g.vector.tensor_copy(o[0], i[0]), [o], [i])
@@ -145,378 +196,300 @@ def rank_program(g, core, T, topo):
 
     def ts(o, a, s1, f0, s2=None, f1=None):
         if f1 is None:
-            op("v", lambda: g.vector.tensor_scalar(o[0], a[0], raw(s1), None, f0), [o], [a, s1])
+            op("v", lambda: g.vector.tensor_scalar(o[0], a[0], s1, None, f0), [o], [a])
         else:
-            op("v", lambda: g.vector.tensor_scalar(o[0], a[0], raw(s1), raw(s2), f0, f1), [o], [a, s1, s2])
+            op("v", lambda: g.vector.tensor_scalar(o[0], a[0], s1, s2, f0, f1), [o], [a])
 
     def fill(o, c):
         op("v", lambda: g.vector.memset(o[0], c), [o], [])
 
-    def scan(o, d, init):
-        one = S("ones", 0, o[3] - o[2])
-        op("v", lambda: g.vector.tensor_tensor_scan(o[0], one[0], d[0], raw(init), Op.mult, Op.add), [o], [one, d, init])
+    def scan(o, d, init, zero=None):
+        z = zero or S("zero", 0, o[1][2] - o[1][1])
+        op("v", lambda: g.vector.tensor_tensor_scan(o[0], z[0], d[0], raw(init), Op.add, Op.add), [o], [z, d, init])
 
-    def act(o, i, f, bias=None, scale=None, acc=None):
-        kw = {}
-        if bias is not None:
-            kw["bias"] = raw(bias)
-        if scale is not None:
-            kw["scale"] = raw(scale)
-        if acc is not None:
-            kw["accum_out"] = acc[0]
-        op("s", lambda: g.scalar.activation(o[0], i[0], f, **kw), [o, acc], [i, bias, scale])
+    def act(o, i, f, bias=0.0, scale=1.0, acc=None):
+        kw = {"accum_out": acc[0]} if acc else {}
+        if bias:
+            kw["bias"] = bias
+        if scale != 1.0:
+            kw["scale"] = scale
+        op("s", lambda: g.scalar.activation(o[0], i[0], f, **kw), [o, acc], [i])
 
-    def mms(items):
-        rd, wr = order("p", [x[0] for x in items], [x[1] for x in items] + [x[2] for x in items])
-        last = None
-        for o, l, x, st, sp in items:
-            last = g.tensor.matmul(o[0], l[0], x[0], st, sp)
-        last.then_inc(T.sem.p, 1)
-        note("p", rd, wr, "p", 1, known["p"])
+    def mms(name, items):
+        outs, ins = [x[0] for x in items], [x[1] for x in items] + [x[2] for x in items]
+
+        def issue():
+            rd, wr = order("p", outs, ins)
+            last = None
+            for o, l, x, st, sp in items:
+                last = g.tensor.matmul(o[0], l[0], x[0], st, sp)
+            last.then_inc(T.sem.p, 1)
+            note("p", rd, wr, "p", 1, known["p"])
+        later(name, outs, ins, issue)
 
     def iota(o, pat, base, cm):
         op("q", lambda: g.iota(o[0], pat, base, cm, allow_small_or_imprecise_dtypes=True), [o], [])
 
-    def select(o, i, pat, f, base, cm):
-        op("q", lambda: g.affine_select(o[0], i[0], pat, f, 0.0, base, cm), [o], [i])
+    def select(o, i, pat, f, base, cm, other=0.0):
+        op("q", lambda: g.affine_select(o[0], i[0], pat, f, other, base, cm), [o], [i])
 
     def band(o, i, t, pat, base, lo, hi):
         select(t, i, pat, Op.is_ge, base - lo, -1)
         select(o, t, [[-a, n] for a, n in pat], Op.is_ge, hi - base, 1)
 
-    def dmas(q, pairs):
+    def dmas(q, name, pairs):
         sem = "dm%d" % ndma[0]
         ndma[0] += 1
-        rd, wr = order(q, [x[0] for x in pairs], [x[1] for x in pairs], True)
-        for o, i in pairs:
-            Q[q].dma_start(raw(o), raw(i)).then_inc(T.sem[sem], 16)
-        note("dma", rd, wr, sem, 16 * len(pairs), known[q])
+        outs, ins = [x[0] for x in pairs], [x[1] for x in pairs]
 
-    def send(src, dsts, dst, sem):
-        order("q", [], [src], True)
-        eng = engine_split(topo, core, dsts)
-        trs = []
-        for d in dsts:
-            rid, pid = topo.addr(d, core)
-            trs.append(RemoteDMATransfer(dst_ids=[DstId(rid=rid, pnc=pid)], dma_engine_mask=sum(1 << x for x in eng[d]),
-                                         remote_sem=T.sem[sem], src=src[0], dst=dst[0]))
-            count["ls"] = count.get("ls", 0) + len(eng[d])
-        g.remote_dma_fused(trs, local_sem=T.sem.ls)
+        def issue():
+            rd, wr = order(q, outs, ins, True)
+            for o, i in pairs:
+                Q[q].dma_start(raw(o), raw(i)).then_inc(T.sem[sem], 16)
+            note("dma", rd, wr, sem, 16 * len(pairs), known[q])
+        later(name, outs, ins, issue)
 
-    def landing(regs, sem, n):
-        if n:
-            note("far", [], spans(regs), sem, n, {})
+    def exchange(src, dst, sem, most=8):
+        def split(c):
+            return engine_split(topo, c, [d for d in cores if d != c], most)
 
-    def tot_dsts(q, rnd):
-        if q == N - 1:
-            return [cores[k] for k in range(N - 1)] if rnd > 0 else []
-        return [cores[k] for k in range(q + 1, N)]
+        def issue():
+            order("q", [], [D(src, q) for q in others], True)
+            eng = split(core)
+            trs = []
+            for q in others:
+                rid, pid = topo.addr(cores[q], core)
+                trs.append(RemoteDMATransfer(dst_ids=[DstId(rid=rid, pnc=pid)], dma_engine_mask=sum(1 << x for x in eng[cores[q]]),
+                                             remote_sem=T.sem[sem], src=T[src][q], dst=T[dst][r]))
+                count["ls"] = count.get("ls", 0) + len(eng[cores[q]])
+            g.remote_dma_fused(trs, local_sem=T.sem.ls)
+            note("far", [], spans([D(dst, q) for q in others]), sem, sum(len(split(cores[q])[core]) for q in others), {})
+        later(sem, [D(dst, q) for q in others], [D(src, q) for q in others], issue)
 
-    def tot(rnd, a, b):
-        return S("tot", 32 * rnd + a, 32 * rnd + b)
-
-    def tot_exchange(rnd):
-        if tot_dsts(r, rnd):
-            send(tot(rnd, 8 * r, 8 * r + 8), tot_dsts(r, rnd), tot(rnd, 8 * r, 8 * r + 8), "at%d" % rnd)
-        frm = [q for q in range(N) if core in tot_dsts(q, rnd)]
-        n = sum(len(engine_split(topo, cores[q], tot_dsts(q, rnd))[core]) for q in frm)
-        landing([tot(rnd, 8 * q, 8 * q + 8) for q in frm], "at%d" % rnd, n)
-
-    def go_exchange(nm, rnd):
-        send(S(nm, 128, 144), [cores[(r + 1) % N]], S(nm, 0, 16), "ag%d" % rnd)
-        landing([S(nm, 0, 16)], "ag%d" % rnd, len(engine_split(topo, cores[(r - 1) % N], [core])[core]))
-
-    eff, pre, kp = S("eff_s", 0, V), S("pre_s", 0, M), S("kp", 0, M)
-
-    def effects(a, b, lst, acc):
-        act(S("e", ECOL[a], ECOL[a] + A * (b - a)), IND(eff, lst), Fn.Identity, acc=acc)
-
-    dmas("y", [(S("ki", 0, 256), T.kid[:])])
-    dmas("s", [(S("todo_s", 0, 128), T.todo[:])])
-    dmas("s", [(eff, T.eff[:])])
-    dmas("y", [(S("mi", 32 * b + 16 * h, 32 * b + 16 * h + 16), T.meth[h:8:2, 512 * b:512 * b + 512])
-               for b in range(4) for h in range(2)])
-    dmas("y", [(pre, T.pre[:])])
-    fill(S("ones", 0, 1024), 1.0)
-    fill(kp, 0.0)
-    fill(S("e", ECOL[0] - 1, ECOL[1], ECOL[1] - ECOL[0]), 0.0)
-    fill(S("e", ECOL[5] - 1, ECOL[5]), 0.0)
-    for k in range(RO):
-        fill(tot(k, 8 * r, 8 * r + 8), 0.0)
-    lin = [[1, 160]]
-    o160, ta, tc = S("ones", 0, 160), S("ta", 0, 160), S("tc", 0, 160)
-    ta8, tc8 = S("ta", 0, 128), S("tc", 0, 128)
-    select(S("e15", 0, 160), o160, [[0, 10], [1, 16]], Op.is_equal, -15, 0)
-    band(S("bp", 0, 160), S("e15", 0, 160), ta, lin, 0, 0, 15)
-    band(S("bg", 0, 128), S("ones", 0, 128), tc8, [[16, 8], [0, 16]], 15, 0, 15)
-    for w, a, b in (("w1", 0, 1024), ("w1", 1024, V), ("w1", V, V + PAD), ("w0", 0, 1024), ("w0", 1024, PAD + LOW)):
-        act(S(w, a, b), S("ones", 0, b - a), Fn.Copy, scale=0.0)
-    act(S("bn", 0, 160), S("bp", 0, 160), Fn.Copy, scale=-1.0)
-    act(S("bgn", 0, 128), S("bg", 0, 128), Fn.Copy, scale=-8192.0)
-    band(S("ns", 0, 160), S("e15", 0, 160), ta, lin, 0, 6, 7)
-    band(S("n1", 0, 160), S("e15", 0, 160), tc, lin, 0, 4, 5)
-    copy(S("rt0", 0, 128), S("todo_s", 0, 128))
-    for a, b in ((0, 1), (1, 5), (5, 8)):
-        effects(a, b, S("rt0", 16 * a, 16 * b), tot(0, 8 * r + a, 8 * r + a + 1))
-    tot_exchange(0)
-    ts(S("k0", 0, 256), S("ki", 0, 256), 4095, Op.bitwise_and)
-    ts(S("ky", 0, 256), S("ki", 0, 256), -1.0, Op.mult, float(EMPTY + 4096 * EMPTY), Op.add)
-    ts(S("kf", 0, 256), S("k0", 0, 256), float(EMPTY), Op.not_equal, 1.0 / 4096, Op.max)
-    tt(S("kz", 0, 256), S("ky", 0, 256), S("kf", 0, 256), Op.mult)
-    ts(S("ab", 0, 256), S("kz", 0, 256), 4095, Op.bitwise_and)
-    ts(S("ab", 256, 512), S("kz", 0, 256), 12, Op.arith_shift_right)
-    copy(S("khi", 0, 512), S("ab", 0, 512))
-    ts(S("kn", 0, 512), S("ab", 0, 512), 0.0, Op.is_gt)
-    dmas("y", [(S("kp", 0, M, p=slice(v, 128, 16)), S(nm, c, c + 256))
-               for v, nm, c in [(0, "khi", 0), (2, "khi", 256), (8, "kn", 0), (9, "kn", 256)]])
-    tt(S("klo", 0, 512), S("ab", 0, 512), S("khi", 0, 512), Op.subtract)
-    dmas("y", [(span(S("kp", 0, M, p=slice(v, 128, 16)), M, M + 1), S("klo", c, c + 256)) for v, c in [(1, 0), (3, 256)]])
-    kp = span(kp, 0, M + 1)
-    ts(S("m2", 0, 128), S("mi", 0, 128), 4095, Op.bitwise_and)
-    ts(S("m2", 128, 256), S("mi", 0, 128), 12, Op.arith_shift_right)
-    copy(S("mf", 0, 256), S("m2", 0, 256))
-    op("v", lambda: g.vector.transpose(T.mt[:, 0:256], T.mf[:, 0:256]), [S("mt", 0, 256)], [S("mf", 0, 256)])
-    copy(S("ml", 0, 256), S("mt", 0, 256))
-    act(S("k3", 2 * M + V, 3 * M), S("w1", 0, V), Fn.Copy)
-    act(S("p0", 0, V), IND(pre, S("ml", 0, 128)), Fn.Identity, bias=-0.25)
-    dmas("y", [(S("k3", M + V * k, M + V * k + V), S("w1", 0, V)) for k in range(2)])
-    fill(S("k3", 2 * M, 2 * M + V), 0.0)
-    fill(S("nb", 0, 2), 0.0)
-    fill(S("tb", 0, 2), 0.0)
-    ts(S("stl", 0, NE * A, A), S("ones", 0, NE), 0.0, Op.mult)
-    copy(S("rf", 0, 128), S("todo_s", 0, 128))
-    tt(S("ds", 0, 160), S("n1", 0, 160), S("ns", 0, 160), Op.subtract)
-    ts(S("p1", 0, P1V), IND(pre, S("ml", 128, 128 + P1V // 16)), -0.25, Op.add)
-    ptab = [S("p0", 0, V), S("p1", 0, V)]
+    eff, kp, pre = S("eff_s", 0, V), S("k3", M, 2 * M), S("k3", 2 * M, 3 * M)
+    i32, rot = S("iw", 0, 128), S("iw", 128 - B, 256 - B)
+    base = S("ps_o", 0, 1)
     cn = ["c0", "c1"]
 
-    def kid_tables():
-        act(S("k3", 0, V), IND(kp, S("ml", 0, 128)), Fn.Identity)
-        copy(S("k3", V, M), IND(kp, S("ml", 128, 256)))
-        dmas("y", [(span(S("k3", 0, V, p=slice(10 + v, 128, 16)), 3 * M, 3 * M + 1), span(S("k3", V, M, p=slice(8 + v, 128, 16)), 0, M))
-                   for v in range(2)])
-        dmas("y", [(S("k3", M * k, M * k + M, p=slice(2 * k + v, 128, 16)), S("k3", 0, M, p=slice(v, 128, 16)))
-                   for k in (1, 2) for v in range(4)])
-        act(S("p1", P1V, V), IND(pre, S("ml", 128 + P1V // 16, 256)), Fn.Identity, bias=-0.25)
+    def zeros(name, lo, hi):
+        for a in range(lo, hi, 512):
+            act(S(name, a, min(hi, a + 512)), S("one32", 0, min(hi - a, 512)), Fn.Copy, scale=0.0)
 
-    def constants():
-        pat = [[16, 8], [2, 16]]
-        iota(S("one32", 0, 128), [[0, 128]], 1, 0)
-        select(S("i32", 0, 128), S("one32", 0, 128), [[1, 128]], Op.is_equal, 0, -1)
-        iota(S("fc", 0, 64), [[16, 64]], 4096, 1)
-        iota(ta8, [[0, 64], [4096, 2]], 0, 0)
-        select(S("sh", 0, 128), ta8, [[1, 128]], Op.is_equal, -1, -1)
-        iota(tc8, [[0, 128]], 2048, 0)
-        select(S("i2k", 0, 128), tc8, [[1, 128]], Op.is_equal, 0, -1)
-        for a in range(2):
-            select(S("mm", 128 * a, 128 * a + 128), S("bg", 0, 128), [[-16, 8], [-2, 16]], Op.is_ge, 16 * a, 1)
-            select(S("mm", 256 + 128 * a, 384 + 128 * a), S("bg", 0, 128), pat, Op.is_gt, -16 * a, -1)
-            band(S("mm", 512 + 128 * a, 640 + 128 * a), S("bgn", 0, 128), (ta8, tc8)[a], pat, -16 * a, -1, 0)
-        select(ta, o160, [[0, 10], [-1, 16]], Op.is_ge, 3, 0)
-        band(S("cv", 0, 160), ta, tc, [[16, 10], [2, 16]], -16, -1, 0)
-        for j in range(3):
-            select(S("cv", 160 * j + 160, 160 * j + 320), S("cv", 0, 160), [[0, 10], [-1, 16]], Op.is_ge, j, 0)
-            select(S("cv", 160 * j + 640, 160 * j + 800), S("cv", 0, 160), [[0, 10], [1, 16]], Op.is_ge, -j - 1, 0)
+    def effects(a, b, rt, j, start):
+        t = S("tot", j, j + 1)
+        act(S("e", PAD + A * a, PAD + A * b), IND(eff, S(rt, 16 * a, 16 * b)), Fn.Identity, acc=t)
+        mms("sum%d" % j, [(base, S("lm", 0, 128), t, start, j == 1)])
+
+    dmas("s", "todo out", [(D("tst", 0, N), T.todo[:])])
+    dmas("y", "meth", [(S("mi", 16 * h, 16 * h + 16), T.meth[2 * r + h, :]) for h in range(2)])
+    dmas("y", "kid", [(S("ki", 0, 128, p=slice(64 * s, 64 * s + 64)), T.kid[2 * r:2 * r + 2, :]) for s in range(2)])
+    dmas("y", "pre", [(S("k3", 2 * M, 3 * M, p=blk(s)), T.pre[blk(r), :]) for s in range(N)])
+    dmas("y", "eff", [(S("eff_s", 0, V, p=blk(s)), T.eff[blk(r), :]) for s in range(N)])
+    dmas("s", "todo own", [(D("tld", r), T.todo[blk(r), :])])
+    exchange("tst", "tld", "at", 4)
+    dmas("y", "todo in", [(S("todo_s", 0, 128), D("tld", 0, N))])
+    fill(S("one32", 0, 512), 1.0)
+    fill(S("zero", 0, 256), 0.0)
+    fill(S("k3", M + 512, 2 * M), 0.0)
+    zeros("k3", M, M + 512)
+    zeros("w", SPARE, W0 + V)
+    act(S("ones", 0, 160), S("one32", 0, 160), Fn.Copy)
+    for nm, a, b in (("e", 0, PAD), ("nb", 0, 2), ("tb", 0, 2), ("ct", 0, 8), ("ct", 264, 272)):
+        iota(S(nm, a, b), [[0, b - a]], 0, 0)
+    select(S("iw", 0, 256), S("one32", 0, 256), [[0, 2], [1, 128]], Op.is_equal, 0, -1)
+    ts(S("m2", 0, 32), S("mi", 0, 32), 4095, Op.bitwise_and)
+    ts(S("m2", 32, 64), S("mi", 0, 32), 12, Op.arith_shift_right)
+    copy(S("mf", 32, 96), S("m2", 0, 64))
+    act(S("mf", 0, 32), S("mf", 32, 64), Fn.Copy)
+    act(S("mf", 96, 128), S("mf", 64, 96), Fn.Copy)
+    mms("methods", [(S("ps_v1", 0, 128), S("mf", 0, 128), i32, True, True)])
+    copy(S("ml", 0, 128), S("ps_v1", 0, 128))
+    ts(S("k0", 0, 128), S("ki", 0, 128), 4095, Op.bitwise_and)
+    ts(S("ky", 0, 128), S("ki", 0, 128), -1.0, Op.mult, float(EMPTY + 4096 * EMPTY), Op.add)
+    ts(S("kf", 0, 128), S("k0", 0, 128), float(EMPTY), Op.not_equal, 1.0 / 4096, Op.max)
+    tt(S("kz", 0, 128), S("ky", 0, 128), S("kf", 0, 128), Op.mult)
+    ts(S("ab", 0, 128), S("kz", 0, 128), 4095, Op.bitwise_and)
+    ts(S("ab", 128, 256), S("kz", 0, 128), 12, Op.arith_shift_right)
+    copy(S("khi", 0, 256), S("ab", 0, 256))
+    tt(S("klo", 0, 256), S("ab", 0, 256), S("khi", 0, 256), Op.subtract)
+    for nm, v in (("khi", 0), ("klo", 1)):
+        dmas("y", nm + " rows", [(S("k3", M, 2 * M, p=row(v + 2 * j, 64 * s, 64 * s + 64)), S(nm, 128 * j, 128 * j + 128))
+                                 for j in range(2) for s in range(2)])
+    lin, pat = [[1, 160]], [[16, 8], [2, 16]]
+    o160, lm = S("ones", 0, 160), S("lm", 0, 128)
+
+    def tmp(j, n=160):
+        return S("ta", 160 * j, 160 * j + n)
+    iota(lm, [[0, 128]], 0, 0)
+    for k in range(1, N):
+        select(lm, lm, [[1, 128]], Op.not_equal, -B * k, -1, 1.0)
+    for nm, x in (("ip", 1.0), ("im", -1.0), ("i2k", 2048.0)):
+        select(S(nm, 0, 128), S("zero", 0, 128), [[1, 128]], Op.not_equal, 0, -1, x)
+    select(S("e15", 0, 160), o160, [[0, 10], [1, 16]], Op.is_equal, -15, 0)
+    band(S("bp", 0, 160), S("e15", 0, 160), tmp(0), lin, 0, 0, 15)
+    band(S("bg", 0, 128), S("ones", 0, 128), tmp(1, 128), [[16, 8], [0, 16]], 15, 0, 15)
+    for nm, src, n, c in (("bn", "bp", 160, -1.0), ("bgn", "bg", 128, 8192.0)):
+        act(S(nm, 0, n), S(src, 0, n), Fn.Copy, scale=c)
+    iota(S("fc", 0, 128), [[0, 2], [16, 64]], 0, 1)
+    select(S("fc", 0, 128), S("fc", 0, 128), [[1, 2], [0, 64]], Op.is_gt, 0, 0)
+    iota(tmp(2, 128), [[0, 64], [4096, 2]], 0, 0)
+    select(S("sh", 0, 128), tmp(2, 128), [[1, 128]], Op.is_equal, -1, -1)
+    for a in range(2):
+        select(S("mm", 128 * a, 128 * a + 128), S("bg", 0, 128), [[-16, 8], [-2, 16]], Op.is_ge, 16 * a, 1)
+        select(S("mm", 256 + 128 * a, 384 + 128 * a), S("bg", 0, 128), pat, Op.is_gt, -16 * a, -1)
+        band(S("mm", 512 + 128 * a, 640 + 128 * a), S("bgn", 0, 128), tmp(3 + a, 128), pat, -16 * a, -1, 0)
+    select(tmp(5), o160, [[0, 10], [-1, 16]], Op.is_ge, 3, 0)
+    band(S("cv", 0, 160), tmp(5), tmp(6), [[16, 10], [2, 16]], -16, -1, 0)
+    for j in range(3):
+        select(S("cv", 160 * j + 160, 160 * j + 320), S("cv", 0, 160), [[0, 10], [-1, 16]], Op.is_ge, j, 0)
+        select(S("cv", 160 * j + 640, 160 * j + 800), S("cv", 0, 160), [[0, 10], [1, 16]], Op.is_ge, -j - 1, 0)
+    tt(S("nd", 0, 8), S("ip", 0, 128, 16), S("ip", 2, 128, 16), Op.add)
+    tt(S("nd", 16, 24), S("ip", 8, 128, 16), S("ip", 9, 128, 16), Op.add)
+    tt(S("nd", 8, 16), S("nd", 16, 24), S("nd", 0, 8), Op.subtract)
+    copy(S("ih", 0, 128), i32)
+    copy(S("fh", 0, 128), S("fc", 0, 128))
+    mms("gaps", [(S("ps_c%d" % h, 256, 512), S("zero", 0, 128), S("zero", 0, 256), True, True) for h in range(2)])
+    half = [slice(0, 64), slice(64, 128)]
+
+    def by_type(out, win, n):
+        copy(S(out, 0, 16 * n), IND(win, S("ml", 0, n)))
+        act(S(out, 16 * n, V), IND(win, S("ml", n, 128)), Fn.Identity)
+    by_type("cn", pre, 48)
+    for k in range(2):
+        dmas("s", "p%d table" % k, [(S("p%d" % k, 0, V, p=half[j]), S("cn", 0, V, p=half[k])) for j in range(2)])
+    dmas("y", "zero rows", [(S("k3", 2 * M, 3 * M, p=row(v)), S("k3", M, 2 * M, p=row(12 + v))) for v in range(4)])
+    by_type("kt", kp, 64)
+    dmas("y", "count rows", [(S("cn", 0, V, p=row((2 * v, 8 + v)[k], 64 * j, 64 * j + 64)), S("kt", 0, V, p=row(2 * v, 64 * k, 64 * k + 64)))
+                             for k in range(2) for v in range(2) for j in range(2)])
+    dmas("y", "kid table", [(S("k3", V * k, V * k + V, p=half[j]), S("kt", 0, V, p=half[k])) for k in range(2) for j in range(2)])
+    dmas("y", "kid rows", [(S("k3", M * k, M * k + M, p=row(2 * k + v)), S("k3", 0, M, p=row(v))) for k in (1, 2) for v in range(4)]
+         + [(S("k3", M, 2 * M, p=row(v)), S("k3", 0, M, p=row(4 + v))) for v in range(2)])
+    copy(S("rt0", 0, 128), S("todo_s", 0, 128))
+    effects(0, 8, "rt0", 1, True)
+    zeros("zero", 256, V)
 
     for rnd in range(RO):
         rt, last = "rt%d" % rnd, rnd == RO - 1
-        stn = "stf" if last else "stb"
 
-        def lst(a, b):
-            return S(rt, 16 * a, 16 * b)
+        def by_type_of_place(table, a, b):
+            return IND(S(table, 0, V), S(rt, 16 * a, 16 * b))
+
+        def by_matmul(k, a, b, ps):
+            c, o = S("cond", V * k + A * a, V * k + A * b), S(ps, 0, A * (b - a))
+            copy(c, by_type_of_place("p%d" % k, a, b))
+            mms("minus%d%d" % (k, a), [(o, S("im", 0, 128), c, True, False)])
+            mms("plus%d%d" % (k, a), [(o, S("ip", 0, 128), S("stb", A * a, A * b), False, True)])
+            act(S(cn[k], A * a, A * b), o, Fn.Sign, bias=0.5)
 
         def direct(k, a, b):
-            tt(S(cn[k], A * a, A * b), IND(ptab[k], lst(a, b)), S(stn, A * a, A * b), Op.is_le)
-
-        def states(a, b, init):
-            scan(S(stn, A * a, A * b), S("e", ECOL[a] - 1, ECOL[a] - 1 + A * (b - a)), init)
-
-        def count_rows(a, b):
-            act(S("ng", A * a, A * b), IND(span(S("k3", 0, V), 3 * M, 3 * M + 1), lst(a, b)), Fn.Identity)
-
-        def rows_to_list(ps, sel, src, h, start, stop):
-            a, b = PARTS[h]
-            mms([(S(ps, a, b), S(sel, 15 - k, 143 - k), S(src, 16 * a + k, 16 * b, 16), start and k == 0, stop and k == 15)
-                 for k in range(16)])
+            tt(S(cn[k], A * a, A * b), by_type_of_place("p%d" % k, a, b), S("stb", A * a, A * b), Op.is_le)
 
         def counts(h):
-            rows_to_list("ps_n", "ns", "ng", h, True, True)
-            rows_to_list("ps_d", "ds", "ng", h, True, True)
+            pc, ct = "ps_c%d" % h, 264 * h + 8
+            mms("counts%d" % h, [(S(pc, 256 + k, 512, 16), S("ng", 1024 * h + k, 1024 * h + 1024, 8), S("nd", 0, 16), True, True) for k in range(8)])
+            act(S("ct", ct, ct + 256), S(pc, 256, 512), Fn.Copy)
+            mms("turn%d" % h, [(S(pc, 64 * j, 64 * j + 64), S("ct", ct + 128 * j - 8 * u, ct + 128 * j - 8 * u + 128), S("ip", u, 128, 2), u == 0, u == 1)
+                               for j in (1, 0) for u in range(2)])
 
         def votes(k, h):
-            rows_to_list("ps_v%d" % h, ("bn", "bp")[k], cn[k], h, k == 0, k == 1)
-
-        def heads(h):
             a, b = PARTS[h]
-            mms([(S("ps_i%d" % h, a, b), S("i32", 0, 128), S("rf", a, b), True, False),
-                 (S("ps_s%d" % h, 64 + a // 2, 64 + b // 2), S("i32", 0, 128), S("fc", a // 2, b // 2), True, False)])
-
-        def first_counts(h):
-            a, b = PARTS[h]
-            act(S("nb", 2 + a, 2 + b), S("ps_n", a, b), Fn.Identity)
-            mms([(S("ps_i%d" % h, a, b), S("sh", 0, 128), S("nb", 2 + a, 2 + b), False, False)]
-                + [(S("ps_s%d" % h, 64 + a // 2, 64 + b // 2), S("mm", 512 + 128 * j, 640 + 128 * j), S("nb", 2 + a + j, 2 + b + j, 2), False, False)
-                   for j in range(2)])
+            mms("votes%d%d" % (k, h), [(S("ps_v%d" % h, a, b), S(("bn", "bp")[k], 15 - j, 143 - j), S(cn[k], 16 * a + j, 16 * b, 16),
+                                        k == 0 and j == 0, k == 1 and j == 15) for j in range(16)])
 
         def choose(h):
             a, b = PARTS[h]
-            pi, ps = "ps_i%d" % h, "ps_s%d" % h
+            pi, pc = "ps_i%d" % h, "ps_c%d" % h
             ts(S("ch", a, b), S("ps_v%d" % h, a, b), 0.0, Op.is_gt)
-            mms([(S(pi, a, b), S("i2k", 0, 128), S("ch", a, b), False, False)])
-            tt(S("tb", 2 + a, 2 + b), S("ch", a, b), S("ps_d", a, b), Op.mult)
-            mms([(S(pi, a, b), S("sh", 0, 128), S("tb", 2 + a, 2 + b), False, True)])
-            mms([(S(ps, 64 + a // 2, 64 + b // 2), S("mm", 512 + 128 * j, 640 + 128 * j), S("tb", 2 + a + j, 2 + b, 2), False, j == 1)
-                 for j in range(2)]
-                + [(S(ps, a // 2, b // 2), S("mm", 128 * j, 128 * j + 128), S(nm, a + j, b + j - 1, 2), nm == "nb" and j == 0, nm == "tb" and j == 3)
-                   for nm in ("nb", "tb") for j in range(4)])
+            tt(S("tb", 2 + a, 2 + b), S("ch", a, b), S(pc, 64, 128), Op.mult)
+            act(S("nb", 2 + a, 2 + b), S(pc, 0, 64), Fn.Copy)
+            mms("first%d" % h, [(S(pi, a, b), S("sh", 0, 128), S("nb", 2 + a, 2 + b), False, False)])
+            mms("index%d" % h, [(S(pi, a, b), S("i2k", 0, 128), S("ch", a, b), False, False),
+                                (S(pi, a, b), S("sh", 0, 128), S("tb", 2 + a, 2 + b), False, True)])
+            copy(S("il", a, b), S(pi, a, b))
 
-        def kid_list(h):
-            a, b = PARTS[h]
-            copy(S("il", a, b), S("ps_i%d" % h, a, b))
-
-        def starts(h):
-            a, b = PARTS[h][0] // 2, PARTS[h][1] // 2
-            scan(S("sta", a, b), S("ps_s%d" % h, a, b), S("sta", a - 1, a) if a else 0.0)
-            tt(S("of", a, b), S("sta", a, b), S("ps_s%d" % h, 64 + a, 64 + b), Op.max)
-            copy(S("ol", a, b), S("of", a, b))
-
-        def kids(j):
-            act(S("kg", 512 * j, 512 * j + 512), IND(span(S("k3", 0, 3 * M), 0, 3 * M + 1), S("il", 32 * j, 32 * j + 32)), Fn.Identity)
+        def starts():
+            for nm in ("nb", "tb"):
+                mms("steps " + nm, [(S("ps_s", 0, 64), S("mm", 128 * j, 128 * j + 128), S(nm, j, 127 + j, 2), False, False) for j in range(4)]
+                    + [(S("ps_s", 64, 128), S("mm", 512 + 128 * j, 640 + 128 * j), S(nm, 2 + j, 129 + j, 2), False, nm == "tb" and j == 1)
+                       for j in range(2)])
+            scan(S("sta", 0, 64), S("ps_s", 0, 64), float(W0))
+            tt(S("of", 0, 64), S("sta", 0, 64), S("ps_s", 64, 128), Op.min)
+            copy(S("ol", 0, 64), S("of", 0, 64))
 
         def place(j):
-            tt(IND(S("w1" if j else "w0", PAD, WIN), S("ol", 16 * j, 16 * j + 16)), S("kg", 512 * j, 512 * j + 512, 2),
-               S("kg", 512 * j + 1, 512 * j + 512, 2), Op.add)
+            lo, hi = 512 * j, 512 * j + 512
+            tt(IND(S("w", 0, W0 + (M if j else LOW)), S("ol", 16 * j, 16 * j + 16)), S("kg", lo, hi, 2), S("kg", lo + 1, hi, 2), Op.add)
 
-        def row_list(ps, w, a, start, stop):
-            o = S(ps, a, a + 64)
+        def row_list(ps, a):
+            o, c = S(ps, a, a + 64), W0 + 16 * a
             items = []
             for k in range(16):
                 j = 0 if k < 13 else 16 - k
-                items.append((o, S("cv", 160 * j + 16 - k, 160 * j + 144 - k), S(w, PAD + 16 * a + k, PAD + 16 * a + 1024, 16), start and k == 0, False))
+                items.append((o, S("cv", 160 * j + 16 - k, 160 * j + 144 - k), S("w", c + k, c + 1024, 16), k == 0, False))
             for k in (13, 14, 15):
                 j = 19 - k
-                items.append((o, S("cv", 160 * j + 32 - k, 160 * j + 160 - k), S(w, 16 * a + k, 16 * a + 1024, 16), False, stop and k == 15))
-            mms(items)
+                items.append((o, S("cv", 160 * j + 32 - k, 160 * j + 160 - k), S("w", c - 16 + k, c + 1008, 16), False, k == 15))
+            mms("row%d" % a, items)
 
-        if rnd == 0:
-            constants()
-            scan(S("offs", 0, 8 * r + 5), tot(0, 0, 8 * r + 5), 0.0)
-            states(0, 1, S("offs", 8 * r - 1, 8 * r) if r else 0.0)
-            states(1, 5, S("offs", 8 * r, 8 * r + 1))
-            states(5, 8, S("offs", 8 * r + 4, 8 * r + 5))
-            kid_tables()
-            heads(0)
-            heads(1)
-            direct(0, 0, 4)
-            votes(0, 0)
-            direct(0, 4, 8)
-            votes(0, 1)
-            count_rows(0, 4)
-            counts(0)
-            count_rows(4, 6)
-            direct(1, 0, 4)
-            first_counts(0)
-            count_rows(6, 8)
-            votes(1, 0)
-            direct(1, 4, 6)
-            choose(0)
-            counts(1)
-            kid_list(0)
-            first_counts(1)
-            kids(1)
-            direct(1, 6, 8)
-            starts(0)
-        else:
-            def off(s):
-                if s == 0:
-                    return S("offs", 8 * r - 2, 8 * r - 1) if r else 0.0
-                return S("offs", 8 * r - 2 + s, 8 * r - 1 + s) if (r or s > 1) else tot(rnd, 31, 32)
+        def types(o, i):
+            ts(o, i, -1.0, Op.mult, float(EMPTY), Op.add)
 
-            def local(s):
-                scan(S("stl", A * (s - 1) + 1, A * s), S("e", ECOL[s], ECOL[s] + A - 1), 0.0)
+        def leaving(a, name):
+            act(S("arr", a, a + 16), S("ps_c0", 112, 128), Fn.Identity, bias=float(EMPTY), scale=-1.0)
+            mms(name, [(S("ps_v1", 0, 16), rot, S("arr", a, a + 16), True, True)])
 
-            def diff(k, a, b):
-                tt(S(("d0", "d1")[k], A * (a - 1), A * (b - 1)), IND(ptab[k], lst(a, b)), S("stl", A * (a - 1), A * (b - 1)), Op.subtract)
-
-            def sign(k, s):
-                act(S(cn[k], A * s, A * s + A), S(("d0", "d1")[k], A * (s - 1), A * s), Fn.Sign, bias=off(s), scale=-1.0)
-
-            for s in range(1, 5):
-                effects(s, s + 1, lst(s, s + 1), tot(rnd, 8 * r + s - 1, 8 * r + s))
-            e56, t56 = S("e", ECOL[5], ECOL[7]), tot(rnd, 8 * r + 4, 8 * r + 5)
-            op("v", lambda: g.vector.tensor_reduce(t56[0], e56[0], Ax.X, Op.add), [t56], [e56])
-            tot_exchange(rnd)
-            iota(S("w1", 0, PAD + V), [[0, PAD + V]], 0, 0)
-            iota(S("w0", 0, PAD + LOW), [[0, PAD + LOW]], 0, 0)
-            local(1)
-            diff(0, 1, 2)
-            local(2)
-            diff(1, 1, 3)
-            effects(0, 1, lst(0, 1), None)
-            count_rows(0, 4)
-            count_rows(4, 8)
-            local(3)
-            local(4)
-            diff(0, 2, 5)
-            copy(S("rf", 0, 128), S(rt, 0, 128))
-            heads(0)
-            heads(1)
-            counts(0)
-            diff(1, 3, 5)
-            scan(S("offs", 0, 8 * r + 4), tot(rnd, 0, 8 * r + 4), tot(rnd, 31, 32))
-            states(0, 1, off(0))
-            states(5, 8, off(5))
-            direct(0, 0, 1)
-            direct(1, 0, 1)
-            first_counts(0)
-            counts(1)
-            for k in range(2):
-                for s in range(1, 4):
-                    sign(k, s)
-                votes(k, 0)
-            first_counts(1)
-            direct(0, 5, 8)
-            sign(0, 4)
-            sign(1, 4)
-            direct(1, 5, 6)
-            choose(0)
-            votes(0, 1)
-            kid_list(0)
-            kids(1)
-            direct(1, 6, 8)
-            starts(0)
-        votes(1, 1)
-        kids(0)
-        choose(1)
-        kid_list(1)
-        kids(2)
-        kids(3)
-        place(1)
-        starts(1)
-        place(2)
-        place(3)
-        row_list("ps_n", "w1", 64, True, True)
-        row_list("ps_d", "w1", 0, True, False)
+        scan(S("stb", 0, V), S("e", PAD - 1, PAD - 1 + V), base, None if rnd else S("w", W0, W0 + V))
+        if rnd:
+            iota(S("w", SPARE, W0 + V), [[0, PAD + V]], 0, 0)
+        if last:
+            mms("eights", [(S("ps_o", 256, 512), S("ip", 0, 128), S("e", PAD - 8 + u, PAD - 8 + V, 8), u == 0, u == 7) for u in range(8)])
+            scan(S("ysb", 0, 256), S("ps_o", 256, 512), base)
+            dmas("y", "ys out", [(D("yst", 0, N), S("ysb", 0, 256))])
+            dmas("y", "ys own", [(T.ys[blk(r), :], S("ysb", 0, 256, p=blk(r)))])
+            exchange("yst", "yld", "ay")
+            dmas("y", "ys in", [(T.ys[blk(q), :], D("yld", q)) for q in others])
+        for x in FAR:
+            by_matmul(*x)
+        for k in range(2):
+            direct(k, 4, NEAR)
+            direct(k, 0, 4)
+        ts(S("ng", 6 * A, V), by_type_of_place("cn", 6, 8), 0.0, Op.is_gt)
+        for a, b in ((4, 6), (0, 4)):
+            act(S("ng", A * a, A * b), by_type_of_place("cn", a, b), Fn.Sign)
+        copy(S("rf", 0, 128), S(rt, 0, 128))
+        mms("heads", [(S("ps_i%d" % h, a, b), S("ih", 0, 128), S("rf", a, b), True, False) for h, (a, b) in enumerate(PARTS)]
+            + [(S("ps_s", 0, 128), S("ih", 0, 128), S("fh", 0, 128), True, False)])
+        for h in (1, 0):
+            counts(h)
+            votes(0, h)
+            votes(1, h)
+            choose(h)
+        starts()
+        for j in (2, 3, 1, 0):
+            act(S("kg", 512 * j, 512 * j + 512), IND(S("k3", 0, 3 * M), S("il", 32 * j, 32 * j + 32)), Fn.Identity)
+        for j in (2, 3, 1):
+            place(j)
+        row_list("ps_c0", 64)
         place(0)
-        row_list("ps_d", "w0", 0, False, True)
+        row_list("ps_c1", 0)
         if not last:
+            phase[0] += 1
             nxt = "rt%d" % (rnd + 1)
-            ts(S(nxt, 80, 144), S("ps_n", 64, 128), -1.0, Op.mult, float(EMPTY), Op.add)
-            go_exchange(nxt, rnd)
-            effects(7, 8, S(nxt, 112, 128), tot(rnd + 1, 8 * r + 6, 8 * r + 7))
-            effects(8, 9, S(nxt, 128, 144), tot(rnd + 1, 8 * r + 7, 8 * r + 8))
-            copy(S("e", ECOL[5], ECOL[7]), IND(eff, S(nxt, 80, 112)))
-            ts(S(nxt, 16, 80), S("ps_d", 0, 64), -1.0, Op.mult, float(EMPTY), Op.add)
+            leaving(0, "rotate")
+            types(S(nxt, 80, 128), S("ps_c0", 64, 112))
+            copy(S(nxt, 0, 16), S("ps_v1", 0, 16))
+            types(S(nxt, 16, 80), S("ps_c1", 0, 64))
+            effects(5, 8, nxt, 0, True)
+            effects(0, 5, nxt, 1, False)
         else:
-            act(S("ysb", 0, 32), S("stf", 0, A, 8), Fn.Identity)
-            act(S("ysb", 160, 256), S("stf", 5 * A, V, 8), Fn.Identity)
-            act(S("fin", 80, 144), S("ps_n", 64, 128), Fn.Identity, bias=float(EMPTY), scale=-1.0)
-            go_exchange("fin", rnd)
-            for s in range(1, 5):
-                ts(S("ysb", 32 * s, 32 * s + 32), S("stl", A * (s - 1), A * s, 8), off(s), Op.add)
-            dmas("s", [(T.ys[:], S("ysb", 0, 256))])
-            ts(S("fin", 16, 80), S("ps_d", 0, 64), -1.0, Op.mult, float(EMPTY), Op.add)
-            dmas("y", [(T.yp[:, 16:128], S("fin", 16, 128))])
-            dmas("y", [(T.yp[:, 0:16], S("fin", 0, 16))])
+            leaving(16, "rotate out")
+            act(S("fin", 80, 128), S("ps_c0", 64, 112), Fn.Identity, bias=float(EMPTY), scale=-1.0)
+            act(S("fin", 0, 16), S("ps_v1", 0, 16), Fn.Copy)
+            types(S("fin", 16, 80), S("ps_c1", 0, 64))
+            dmas("y", "yp out", [(D("pst", 0, N), S("fin", 0, 128))])
+            dmas("s", "yp own", [(T.yp[blk(r), :], S("fin", 0, 128, p=blk(r)))])
+            exchange("pst", "pld", "ap")
+            dmas("y", "yp in", [(T.yp[B * a:B * b, :], D("pld", a, b)) for a, b in ((0, r), (r + 1, N)) if a < b])
+    issue_all()
     for sem in count:
         g.wait_ge(T.sem[sem], count[sem])

from concourse.bass import DstId, RemoteDMATransfer
from concourse.mybir import AluOpType as Op, ActivationFunctionType as Fn

V, A, M, RO, N = 2048, 256, 4096, 3, 4
B = 128 // N
EMPTY = V - 1
PAD = 16
SPARE = 1152
W0 = SPARE + PAD
LOW = 1021
PARTS = [(0, 64), (64, 128)]
NEAR = 5
FAR = [(0, 6, 8, "ps_v0"), (1, 6, 8, "ps_s"), (0, 5, 6, "ps_i0"), (1, 5, 6, "ps_i1")]

START = """todo out, meth, kid, pre, eff, todo own, one32:0, k3:4096, k3:4608, zero:0, e:0, ct:0, ct:264, iw:0, nb:0, tb:0, ones:0,
    w:1152, w:1664, w:2176, w:2688, w:3200, at, gaps,
    m2:0, m2:32, mf:32, mf:0, mf:96, k0:0, ky:0, kf:0, kz:0, methods, ab:128, ab:0, khi:0, khi rows, ml:0, klo:0, klo rows,
    cn:768, cn:0, p0 table, p1 table, todo in, ih:0,
    lm:0, ip:0, im:0, fc:0, e15:0, ta:160, ta:0, bg:0, bp:0, i2k:0, ta:320, mm:128, sh:0, mm:0, mm:256, mm:384,
    nd:0, nd:16, nd:8, zero rows, kt:0, kt:1024, fh:0, bn:0, bgn:0,
    ta:480, ta:640, mm:512, mm:640, ta:800, ta:960, cv:0, cv:960, cv:320, cv:800, cv:160, cv:640, cv:480,
    rt:0, count rows, kid table, kid rows"""
ROUND = """rt:80, arr:0, cond:1536, e:1296, rotate, w:1152, rt:16, rt:0, cond:3328, e:16, sum0, cond:3584, minus16, minus15,
    cond:1280, ng:1536, ng:1024, sum1, rf:0, stb:0, ng:0, counts1, minus05, minus06, c0:1024, plus06, c0:0, plus05, plus15,
    c0:1536, c0:1280, plus16, eights, counts0, c1:1024, c1:1536, votes01, c1:0, c1:1280, votes00, ct:272, ct:8, votes11,
    turn1, turn0, ch:64, votes10, nb:2, tb:66, ysb:0, nb:66, heads, ys out, ys own, ay, ys in, first0, ch:0, first1, index1,
    steps nb, tb:2, il:64, steps tb, kg:1024, index0, sta:0, of:0, il:0, ol:0, kg:1536, w:32, kg:512, w:48, kg:0, w:16,
    zero:256, zero:768, zero:1280, zero:1792, row64, w:0, arr:16, fin:80, row0, rotate out, fin:0, fin:16,
    yp out, yp own, ap, yp in"""

SCRATCH = {
    "todo_s": ("sbuf", [128, 128], "int32"), "mi": ("sbuf", [128, 32], "int32"), "m2": ("sbuf", [128, 64], "int32"),
    "mf": ("sbuf", [128, 128], "float32"), "ml": ("sbuf", [128, 128], "uint16"),
    "ki": ("sbuf", [128, 128], "int32"), "ky": ("sbuf", [128, 128], "float32"), "k0": ("sbuf", [128, 128], "int32"),
    "kf": ("sbuf", [128, 128], "float32"), "kz": ("sbuf", [128, 128], "int32"), "ab": ("sbuf", [128, 256], "int32"),
    "khi": ("sbuf", [128, 256], "bfloat16"), "klo": ("sbuf", [128, 256], "bfloat16"),
    "eff_s": ("sbuf", [128, V], "bfloat16"), "k3": ("sbuf", [128, 3 * M], "bfloat16"),
    "p0": ("sbuf", [128, V], "bfloat16"), "p1": ("sbuf", [128, V], "bfloat16"),
    "cn": ("sbuf", [128, V], "bfloat16"), "kt": ("sbuf", [128, V], "bfloat16"),
    "e": ("sbuf", [128, PAD + V], "bfloat16"), "stb": ("sbuf", [128, V], "bfloat16"), "cond": ("sbuf", [128, 2 * V], "bfloat16"),
    "c0": ("sbuf", [128, V], "bfloat16"), "c1": ("sbuf", [128, V], "bfloat16"),
    "ng": ("sbuf", [128, V], "bfloat16"), "kg": ("sbuf", [128, V], "bfloat16"),
    "w": ("sbuf", [128, W0 + M], "bfloat16"), "zero": ("sbuf", [128, V], "bfloat16"), "ones": ("sbuf", [128, 160], "bfloat16"),
    "rt0": ("sbuf", [128, 128], "uint16"), "rt1": ("sbuf", [128, 128], "uint16"), "rt2": ("sbuf", [128, 128], "uint16"),
    "rf": ("sbuf", [128, 128], "float16"), "fin": ("sbuf", [128, 128], "float32"), "ysb": ("sbuf", [128, 256], "float32"),
    "tot": ("sbuf", [128, 2], "float32"), "arr": ("sbuf", [128, 32], "float32"), "ct": ("sbuf", [128, 2 * 264], "bfloat16"),
    "ch": ("sbuf", [128, 128], "bfloat16"), "nb": ("sbuf", [128, 136], "bfloat16"), "tb": ("sbuf", [128, 136], "bfloat16"),
    "il": ("sbuf", [128, 128], "uint16"), "sta": ("sbuf", [128, 64], "float32"), "of": ("sbuf", [128, 64], "float32"),
    "ol": ("sbuf", [128, 64], "uint16"),
    "tst": ("dram", [N, 128, 32], "int32"), "tld": ("dram", [N, 128, 32], "int32"),
    "yst": ("dram", [N, 128, 64], "float32"), "yld": ("dram", [N, 128, 64], "float32"),
    "pst": ("dram", [N, 128, 32], "float32"), "pld": ("dram", [N, 128, 32], "float32"),
    "e15": ("sbuf", [128, 160], "bfloat16"), "bp": ("sbuf", [128, 160], "bfloat16"), "bn": ("sbuf", [128, 160], "bfloat16"),
    "nd": ("sbuf", [128, 24], "bfloat16"), "cv": ("sbuf", [128, 7 * 160], "bfloat16"), "i2k": ("sbuf", [128, 128], "bfloat16"),
    "ip": ("sbuf", [128, 128], "bfloat16"), "im": ("sbuf", [128, 128], "bfloat16"), "ih": ("sbuf", [128, 128], "float16"),
    "sh": ("sbuf", [128, 128], "bfloat16"), "bg": ("sbuf", [128, 128], "bfloat16"), "bgn": ("sbuf", [128, 128], "bfloat16"),
    "ta": ("sbuf", [128, 7 * 160], "bfloat16"), "one32": ("sbuf", [128, 512], "float32"),
    "mm": ("sbuf", [128, 6 * 128], "bfloat16"), "fc": ("sbuf", [128, 128], "float32"), "fh": ("sbuf", [128, 128], "float16"),
    "iw": ("sbuf", [128, 256], "float32"), "lm": ("sbuf", [128, 128], "float32"),
    "ps_c0": ("psum", [128, 512], "float32"), "ps_c1": ("psum", [128, 512], "float32"),
    "ps_v0": ("psum", [128, 512], "float32"), "ps_i0": ("psum", [128, 512], "float32"), "ps_s": ("psum", [128, 512], "float32"),
    "ps_v1": ("psum", [128, 512], "float32"), "ps_i1": ("psum", [128, 512], "float32"), "ps_o": ("psum", [128, 512], "float32"),
}
SEMAPHORES = ["v", "s", "p", "q", "ls", "at", "ay", "ap"] + ["dm%d" % i for i in range(24)]


def engine_split(topo, src, dsts, most):
    near = [d for d in dsts if d in topo.cores_of(src)]
    far = [d for d in dsts if d not in near]
    res = {}
    used = set()
    if far:
        pool = topo.engines(src, far[0])
        n = 1
        while 2 * n * len(far) <= len(pool):
            n *= 2
        for i, d in enumerate(far):
            res[d] = pool[i * n:(i + 1) * n]
        used = set(pool)
    for d in near:
        pool = topo.engines(src, d)
        rest = [x for x in pool if x not in used]
        res[d] = rest[len(rest) - len(pool) // 2:]
    return {d: res[d][::max(1, len(res[d]) // most)] for d in res}


def rank_program(g, core, T, topo):
    r = T.rank_of(core)
    if r is None:
        return
    cores = list(T.cores)
    others = [q for q in range(N) if q != r]
    Q = {"v": g.vector, "s": g.scalar, "p": g.tensor, "q": g, "y": g.sync}
    hist = {}
    known = {k: {} for k in Q}
    count = {}
    ndma = [0]
    ALL = (1 << 128) - 1

    def S(name, lo, hi, step=1, p=None):
        ps = slice(None) if p is None else p
        ap = T[name][ps, lo:hi:step] if step != 1 else T[name][ps, lo:hi]
        rows = ALL if p is None else sum(1 << x for x in range(128)[p])
        return (ap, (name, 0, 512, ALL) if name.startswith("ps_") else (name, lo, hi, rows), None)

    def D(name, lo, hi=None):
        return (T[name][lo], (name, lo, lo + 1, ALL), None) if hi is None else (T[name][lo:hi], (name, lo, hi, ALL), None)

    def blk(s):
        return slice(B * s, B * s + B)

    def row(v, lo=0, hi=128):
        return slice(lo + v, hi, 16)

    def IND(win, lst):
        return (win[0].indirect(lst[0]), win[1], lst)

    def spans(xs):
        return [x[1] for x in xs if isinstance(x, tuple)]

    def lists(xs):
        return [x[2][1] for x in xs if isinstance(x, tuple) and x[2]]

    def meet(a, b):
        return a[1] < b[2] and b[1] < a[2] and a[3] & b[3]

    calls = []
    phase = [0]

    def later(name, outs, ins, issue):
        calls.append((spans(ins) + lists(ins) + lists(outs), spans(outs), issue, phase[0], name))

    def issue_all():
        pre, seen = [], {}
        for i, c in enumerate(calls):
            acc = [(a, False) for a in c[0]] + [(a, True) for a in c[1]]
            pre.append(set(j for a, w in acc for b, hw, j in seen.get(a[0], []) if (hw or w) and meet(a, b)))
            for a, w in acc:
                seen.setdefault(a[0], []).append((a, w, i))
        names = [[x.strip() for x in s.split(",")] for s in (START + "," + ROUND, ROUND)]
        left = sorted(range(len(calls)), key=lambda i: (calls[i][3], names[min(calls[i][3], 1)].index(calls[i][4]), i))
        done = set()
        while left:
            i = next(i for i in left if pre[i] <= done)
            left.remove(i)
            done.add(i)
            calls[i][2]()

    def need(q, ev):
        sem, n, snap = ev
        if known[q].get(sem, 0) < n:
            Q[q].wait_ge(T.sem[sem], n)
            known[q][sem] = n
            for k in snap:
                if known[q].get(k, 0) < snap[k]:
                    known[q][k] = snap[k]

    def order(q, outs, ins, dma=False):
        rd = spans(ins) + lists(ins) + lists(outs)
        wr = spans(outs)
        best = {}
        for acc, w in [(a, False) for a in rd] + [(a, True) for a in wr]:
            bank = acc[0].startswith("ps_")
            for b, hw, ev, hq in hist.get(acc[0], []):
                if meet(acc, b):
                    same = hq == q and not dma
                    if ((hw or w) and q != "p" if same else hw or w or bank):
                        if ev[0] not in best or best[ev[0]][1] < ev[1]:
                            best[ev[0]] = ev
        for k in best:
            need(q, best[k])
        return rd, wr

    def note(q, rd, wr, sem, n, seen):
        count[sem] = count.get(sem, 0) + n
        ev = (sem, count[sem], dict(seen))
        for acc, w in [(a, False) for a in rd] + [(a, True) for a in wr]:
            hist.setdefault(acc[0], []).append((acc, w, ev, q))

    def raw(x):
        return x[0] if isinstance(x, tuple) else x

    def op(q, call, outs, ins):
        def issue():
            rd, wr = order(q, outs, ins)
            call().then_inc(T.sem[q], 1)
            note(q, rd, wr, q, 1, known[q])
        o = outs[0][2][1] if outs[0][2] else outs[0][1]
        later("%s:%d" % ("rt" if outs[0][1][0][:2] == "rt" else outs[0][1][0], o[1]), outs, ins, issue)

    def copy(o, i):
        op("v", lambda: g.vector.tensor_copy(o[0], i[0]), [o], [i])

    def tt(o, a, b, f):
        op("v", lambda: g.vector.tensor_tensor(o[0], a[0], b[0], f), [o], [a, b])

    def ts(o, a, s1, f0, s2=None, f1=None):
        if f1 is None:
            op("v", lambda: g.vector.tensor_scalar(o[0], a[0], s1, None, f0), [o], [a])
        else:
            op("v", lambda: g.vector.tensor_scalar(o[0], a[0], s1, s2, f0, f1), [o], [a])

    def fill(o, c):
        op("v", lambda: g.vector.memset(o[0], c), [o], [])

    def scan(o, d, init, zero=None):
        z = zero or S("zero", 0, o[1][2] - o[1][1])
        op("v", lambda: g.vector.tensor_tensor_scan(o[0], z[0], d[0], raw(init), Op.add, Op.add), [o], [z, d, init])

    def act(o, i, f, bias=0.0, scale=1.0, acc=None):
        kw = {"accum_out": acc[0]} if acc else {}
        if bias:
            kw["bias"] = bias
        if scale != 1.0:
            kw["scale"] = scale
        op("s", lambda: g.scalar.activation(o[0], i[0], f, **kw), [o, acc], [i])

    def mms(name, items):
        outs, ins = [x[0] for x in items], [x[1] for x in items] + [x[2] for x in items]

        def issue():
            rd, wr = order("p", outs, ins)
            last = None
            for o, l, x, st, sp in items:
                last = g.tensor.matmul(o[0], l[0], x[0], st, sp)
            last.then_inc(T.sem.p, 1)
            note("p", rd, wr, "p", 1, known["p"])
        later(name, outs, ins, issue)

    def iota(o, pat, base, cm):
        op("q", lambda: g.iota(o[0], pat, base, cm, allow_small_or_imprecise_dtypes=True), [o], [])

    def select(o, i, pat, f, base, cm, other=0.0):
        op("q", lambda: g.affine_select(o[0], i[0], pat, f, other, base, cm), [o], [i])

    def band(o, i, t, pat, base, lo, hi):
        select(t, i, pat, Op.is_ge, base - lo, -1)
        select(o, t, [[-a, n] for a, n in pat], Op.is_ge, hi - base, 1)

    def dmas(q, name, pairs):
        sem = "dm%d" % ndma[0]
        ndma[0] += 1
        outs, ins = [x[0] for x in pairs], [x[1] for x in pairs]

        def issue():
            rd, wr = order(q, outs, ins, True)
            for o, i in pairs:
                Q[q].dma_start(raw(o), raw(i)).then_inc(T.sem[sem], 16)
            note("dma", rd, wr, sem, 16 * len(pairs), known[q])
        later(name, outs, ins, issue)

    def exchange(src, dst, sem, most=8):
        def split(c):
            return engine_split(topo, c, [d for d in cores if d != c], most)

        def issue():
            order("q", [], [D(src, q) for q in others], True)
            eng = split(core)
            trs = []
            for q in others:
                rid, pid = topo.addr(cores[q], core)
                trs.append(RemoteDMATransfer(dst_ids=[DstId(rid=rid, pnc=pid)], dma_engine_mask=sum(1 << x for x in eng[cores[q]]),
                                             remote_sem=T.sem[sem], src=T[src][q], dst=T[dst][r]))
                count["ls"] = count.get("ls", 0) + len(eng[cores[q]])
            g.remote_dma_fused(trs, local_sem=T.sem.ls)
            note("far", [], spans([D(dst, q) for q in others]), sem, sum(len(split(cores[q])[core]) for q in others), {})
        later(sem, [D(dst, q) for q in others], [D(src, q) for q in others], issue)

    eff, kp, pre = S("eff_s", 0, V), S("k3", M, 2 * M), S("k3", 2 * M, 3 * M)
    i32, rot = S("iw", 0, 128), S("iw", 128 - B, 256 - B)
    base = S("ps_o", 0, 1)
    cn = ["c0", "c1"]

    def zeros(name, lo, hi):
        for a in range(lo, hi, 512):
            act(S(name, a, min(hi, a + 512)), S("one32", 0, min(hi - a, 512)), Fn.Copy, scale=0.0)

    def effects(a, b, rt, j, start):
        t = S("tot", j, j + 1)
        act(S("e", PAD + A * a, PAD + A * b), IND(eff, S(rt, 16 * a, 16 * b)), Fn.Identity, acc=t)
        mms("sum%d" % j, [(base, S("lm", 0, 128), t, start, j == 1)])

    dmas("s", "todo out", [(D("tst", 0, N), T.todo[:])])
    dmas("y", "meth", [(S("mi", 16 * h, 16 * h + 16), T.meth[2 * r + h, :]) for h in range(2)])
    dmas("y", "kid", [(S("ki", 0, 128, p=slice(64 * s, 64 * s + 64)), T.kid[2 * r:2 * r + 2, :]) for s in range(2)])
    dmas("y", "pre", [(S("k3", 2 * M, 3 * M, p=blk(s)), T.pre[blk(r), :]) for s in range(N)])
    dmas("y", "eff", [(S("eff_s", 0, V, p=blk(s)), T.eff[blk(r), :]) for s in range(N)])
    dmas("s", "todo own", [(D("tld", r), T.todo[blk(r), :])])
    exchange("tst", "tld", "at", 4)
    dmas("y", "todo in", [(S("todo_s", 0, 128), D("tld", 0, N))])
    fill(S("one32", 0, 512), 1.0)
    fill(S("zero", 0, 256), 0.0)
    fill(S("k3", M + 512, 2 * M), 0.0)
    zeros("k3", M, M + 512)
    zeros("w", SPARE, W0 + V)
    act(S("ones", 0, 160), S("one32", 0, 160), Fn.Copy)
    for nm, a, b in (("e", 0, PAD), ("nb", 0, 2), ("tb", 0, 2), ("ct", 0, 8), ("ct", 264, 272)):
        iota(S(nm, a, b), [[0, b - a]], 0, 0)
    select(S("iw", 0, 256), S("one32", 0, 256), [[0, 2], [1, 128]], Op.is_equal, 0, -1)
    ts(S("m2", 0, 32), S("mi", 0, 32), 4095, Op.bitwise_and)
    ts(S("m2", 32, 64), S("mi", 0, 32), 12, Op.arith_shift_right)
    copy(S("mf", 32, 96), S("m2", 0, 64))
    act(S("mf", 0, 32), S("mf", 32, 64), Fn.Copy)
    act(S("mf", 96, 128), S("mf", 64, 96), Fn.Copy)
    mms("methods", [(S("ps_v1", 0, 128), S("mf", 0, 128), i32, True, True)])
    copy(S("ml", 0, 128), S("ps_v1", 0, 128))
    ts(S("k0", 0, 128), S("ki", 0, 128), 4095, Op.bitwise_and)
    ts(S("ky", 0, 128), S("ki", 0, 128), -1.0, Op.mult, float(EMPTY + 4096 * EMPTY), Op.add)
    ts(S("kf", 0, 128), S("k0", 0, 128), float(EMPTY), Op.not_equal, 1.0 / 4096, Op.max)
    tt(S("kz", 0, 128), S("ky", 0, 128), S("kf", 0, 128), Op.mult)
    ts(S("ab", 0, 128), S("kz", 0, 128), 4095, Op.bitwise_and)
    ts(S("ab", 128, 256), S("kz", 0, 128), 12, Op.arith_shift_right)
    copy(S("khi", 0, 256), S("ab", 0, 256))
    tt(S("klo", 0, 256), S("ab", 0, 256), S("khi", 0, 256), Op.subtract)
    for nm, v in (("khi", 0), ("klo", 1)):
        dmas("y", nm + " rows", [(S("k3", M, 2 * M, p=row(v + 2 * j, 64 * s, 64 * s + 64)), S(nm, 128 * j, 128 * j + 128))
                                 for j in range(2) for s in range(2)])
    lin, pat = [[1, 160]], [[16, 8], [2, 16]]
    o160, lm = S("ones", 0, 160), S("lm", 0, 128)

    def tmp(j, n=160):
        return S("ta", 160 * j, 160 * j + n)
    iota(lm, [[0, 128]], 0, 0)
    for k in range(1, N):
        select(lm, lm, [[1, 128]], Op.not_equal, -B * k, -1, 1.0)
    for nm, x in (("ip", 1.0), ("im", -1.0), ("i2k", 2048.0)):
        select(S(nm, 0, 128), S("zero", 0, 128), [[1, 128]], Op.not_equal, 0, -1, x)
    select(S("e15", 0, 160), o160, [[0, 10], [1, 16]], Op.is_equal, -15, 0)
    band(S("bp", 0, 160), S("e15", 0, 160), tmp(0), lin, 0, 0, 15)
    band(S("bg", 0, 128), S("ones", 0, 128), tmp(1, 128), [[16, 8], [0, 16]], 15, 0, 15)
    for nm, src, n, c in (("bn", "bp", 160, -1.0), ("bgn", "bg", 128, 8192.0)):
        act(S(nm, 0, n), S(src, 0, n), Fn.Copy, scale=c)
    iota(S("fc", 0, 128), [[0, 2], [16, 64]], 0, 1)
    select(S("fc", 0, 128), S("fc", 0, 128), [[1, 2], [0, 64]], Op.is_gt, 0, 0)
    iota(tmp(2, 128), [[0, 64], [4096, 2]], 0, 0)
    select(S("sh", 0, 128), tmp(2, 128), [[1, 128]], Op.is_equal, -1, -1)
    for a in range(2):
        select(S("mm", 128 * a, 128 * a + 128), S("bg", 0, 128), [[-16, 8], [-2, 16]], Op.is_ge, 16 * a, 1)
        select(S("mm", 256 + 128 * a, 384 + 128 * a), S("bg", 0, 128), pat, Op.is_gt, -16 * a, -1)
        band(S("mm", 512 + 128 * a, 640 + 128 * a), S("bgn", 0, 128), tmp(3 + a, 128), pat, -16 * a, -1, 0)
    select(tmp(5), o160, [[0, 10], [-1, 16]], Op.is_ge, 3, 0)
    band(S("cv", 0, 160), tmp(5), tmp(6), [[16, 10], [2, 16]], -16, -1, 0)
    for j in range(3):
        select(S("cv", 160 * j + 160, 160 * j + 320), S("cv", 0, 160), [[0, 10], [-1, 16]], Op.is_ge, j, 0)
        select(S("cv", 160 * j + 640, 160 * j + 800), S("cv", 0, 160), [[0, 10], [1, 16]], Op.is_ge, -j - 1, 0)
    tt(S("nd", 0, 8), S("ip", 0, 128, 16), S("ip", 2, 128, 16), Op.add)
    tt(S("nd", 16, 24), S("ip", 8, 128, 16), S("ip", 9, 128, 16), Op.add)
    tt(S("nd", 8, 16), S("nd", 16, 24), S("nd", 0, 8), Op.subtract)
    copy(S("ih", 0, 128), i32)
    copy(S("fh", 0, 128), S("fc", 0, 128))
    mms("gaps", [(S("ps_c%d" % h, 256, 512), S("zero", 0, 128), S("zero", 0, 256), True, True) for h in range(2)])
    half = [slice(0, 64), slice(64, 128)]

    def by_type(out, win, n):
        copy(S(out, 0, 16 * n), IND(win, S("ml", 0, n)))
        act(S(out, 16 * n, V), IND(win, S("ml", n, 128)), Fn.Identity)
    by_type("cn", pre, 48)
    for k in range(2):
        dmas("s", "p%d table" % k, [(S("p%d" % k, 0, V, p=half[j]), S("cn", 0, V, p=half[k])) for j in range(2)])
    dmas("y", "zero rows", [(S("k3", 2 * M, 3 * M, p=row(v)), S("k3", M, 2 * M, p=row(12 + v))) for v in range(4)])
    by_type("kt", kp, 64)
    dmas("y", "count rows", [(S("cn", 0, V, p=row((2 * v, 8 + v)[k], 64 * j, 64 * j + 64)), S("kt", 0, V, p=row(2 * v, 64 * k, 64 * k + 64)))
                             for k in range(2) for v in range(2) for j in range(2)])
    dmas("y", "kid table", [(S("k3", V * k, V * k + V, p=half[j]), S("kt", 0, V, p=half[k])) for k in range(2) for j in range(2)])
    dmas("y", "kid rows", [(S("k3", M * k, M * k + M, p=row(2 * k + v)), S("k3", 0, M, p=row(v))) for k in (1, 2) for v in range(4)]
         + [(S("k3", M, 2 * M, p=row(v)), S("k3", 0, M, p=row(4 + v))) for v in range(2)])
    copy(S("rt0", 0, 128), S("todo_s", 0, 128))
    effects(0, 8, "rt0", 1, True)
    zeros("zero", 256, V)

    for rnd in range(RO):
        rt, last = "rt%d" % rnd, rnd == RO - 1

        def by_type_of_place(table, a, b):
            return IND(S(table, 0, V), S(rt, 16 * a, 16 * b))

        def by_matmul(k, a, b, ps):
            c, o = S("cond", V * k + A * a, V * k + A * b), S(ps, 0, A * (b - a))
            copy(c, by_type_of_place("p%d" % k, a, b))
            mms("minus%d%d" % (k, a), [(o, S("im", 0, 128), c, True, False)])
            mms("plus%d%d" % (k, a), [(o, S("ip", 0, 128), S("stb", A * a, A * b), False, True)])
            act(S(cn[k], A * a, A * b), o, Fn.Sign, bias=0.5)

        def direct(k, a, b):
            tt(S(cn[k], A * a, A * b), by_type_of_place("p%d" % k, a, b), S("stb", A * a, A * b), Op.is_le)

        def counts(h):
            pc, ct = "ps_c%d" % h, 264 * h + 8
            mms("counts%d" % h, [(S(pc, 256 + k, 512, 16), S("ng", 1024 * h + k, 1024 * h + 1024, 8), S("nd", 0, 16), True, True) for k in range(8)])
            act(S("ct", ct, ct + 256), S(pc, 256, 512), Fn.Copy)
            mms("turn%d" % h, [(S(pc, 64 * j, 64 * j + 64), S("ct", ct + 128 * j - 8 * u, ct + 128 * j - 8 * u + 128), S("ip", u, 128, 2), u == 0, u == 1)
                               for j in (1, 0) for u in range(2)])

        def votes(k, h):
            a, b = PARTS[h]
            mms("votes%d%d" % (k, h), [(S("ps_v%d" % h, a, b), S(("bn", "bp")[k], 15 - j, 143 - j), S(cn[k], 16 * a + j, 16 * b, 16),
                                        k == 0 and j == 0, k == 1 and j == 15) for j in range(16)])

        def choose(h):
            a, b = PARTS[h]
            pi, pc = "ps_i%d" % h, "ps_c%d" % h
            ts(S("ch", a, b), S("ps_v%d" % h, a, b), 0.0, Op.is_gt)
            tt(S("tb", 2 + a, 2 + b), S("ch", a, b), S(pc, 64, 128), Op.mult)
            act(S("nb", 2 + a, 2 + b), S(pc, 0, 64), Fn.Copy)
            mms("first%d" % h, [(S(pi, a, b), S("sh", 0, 128), S("nb", 2 + a, 2 + b), False, False)])
            mms("index%d" % h, [(S(pi, a, b), S("i2k", 0, 128), S("ch", a, b), False, False),
                                (S(pi, a, b), S("sh", 0, 128), S("tb", 2 + a, 2 + b), False, True)])
            copy(S("il", a, b), S(pi, a, b))

        def starts():
            for nm in ("nb", "tb"):
                mms("steps " + nm, [(S("ps_s", 0, 64), S("mm", 128 * j, 128 * j + 128), S(nm, j, 127 + j, 2), False, False) for j in range(4)]
                    + [(S("ps_s", 64, 128), S("mm", 512 + 128 * j, 640 + 128 * j), S(nm, 2 + j, 129 + j, 2), False, nm == "tb" and j == 1)
                       for j in range(2)])
            scan(S("sta", 0, 64), S("ps_s", 0, 64), float(W0))
            tt(S("of", 0, 64), S("sta", 0, 64), S("ps_s", 64, 128), Op.min)
            copy(S("ol", 0, 64), S("of", 0, 64))

        def place(j):
            lo, hi = 512 * j, 512 * j + 512
            tt(IND(S("w", 0, W0 + (M if j else LOW)), S("ol", 16 * j, 16 * j + 16)), S("kg", lo, hi, 2), S("kg", lo + 1, hi, 2), Op.add)

        def row_list(ps, a):
            o, c = S(ps, a, a + 64), W0 + 16 * a
            items = []
            for k in range(16):
                j = 0 if k < 13 else 16 - k
                items.append((o, S("cv", 160 * j + 16 - k, 160 * j + 144 - k), S("w", c + k, c + 1024, 16), k == 0, False))
            for k in (13, 14, 15):
                j = 19 - k
                items.append((o, S("cv", 160 * j + 32 - k, 160 * j + 160 - k), S("w", c - 16 + k, c + 1008, 16), False, k == 15))
            mms("row%d" % a, items)

        def types(o, i):
            ts(o, i, -1.0, Op.mult, float(EMPTY), Op.add)

        def leaving(a, name):
            act(S("arr", a, a + 16), S("ps_c0", 112, 128), Fn.Identity, bias=float(EMPTY), scale=-1.0)
            mms(name, [(S("ps_v1", 0, 16), rot, S("arr", a, a + 16), True, True)])

        scan(S("stb", 0, V), S("e", PAD - 1, PAD - 1 + V), base, None if rnd else S("w", W0, W0 + V))
        if rnd:
            iota(S("w", SPARE, W0 + V), [[0, PAD + V]], 0, 0)
        if last:
            mms("eights", [(S("ps_o", 256, 512), S("ip", 0, 128), S("e", PAD - 8 + u, PAD - 8 + V, 8), u == 0, u == 7) for u in range(8)])
            scan(S("ysb", 0, 256), S("ps_o", 256, 512), base)
            dmas("y", "ys out", [(D("yst", 0, N), S("ysb", 0, 256))])
            dmas("y", "ys own", [(T.ys[blk(r), :], S("ysb", 0, 256, p=blk(r)))])
            exchange("yst", "yld", "ay")
            dmas("y", "ys in", [(T.ys[blk(q), :], D("yld", q)) for q in others])
        for x in FAR:
            by_matmul(*x)
        for k in range(2):
            direct(k, 4, NEAR)
            direct(k, 0, 4)
        ts(S("ng", 6 * A, V), by_type_of_place("cn", 6, 8), 0.0, Op.is_gt)
        for a, b in ((4, 6), (0, 4)):
            act(S("ng", A * a, A * b), by_type_of_place("cn", a, b), Fn.Sign)
        copy(S("rf", 0, 128), S(rt, 0, 128))
        mms("heads", [(S("ps_i%d" % h, a, b), S("ih", 0, 128), S("rf", a, b), True, False) for h, (a, b) in enumerate(PARTS)]
            + [(S("ps_s", 0, 128), S("ih", 0, 128), S("fh", 0, 128), True, False)])
        for h in (1, 0):
            counts(h)
            votes(0, h)
            votes(1, h)
            choose(h)
        starts()
        for j in (2, 3, 1, 0):
            act(S("kg", 512 * j, 512 * j + 512), IND(S("k3", 0, 3 * M), S("il", 32 * j, 32 * j + 32)), Fn.Identity)
        for j in (2, 3, 1):
            place(j)
        row_list("ps_c0", 64)
        place(0)
        row_list("ps_c1", 0)
        if not last:
            phase[0] += 1
            nxt = "rt%d" % (rnd + 1)
            leaving(0, "rotate")
            types(S(nxt, 80, 128), S("ps_c0", 64, 112))
            copy(S(nxt, 0, 16), S("ps_v1", 0, 16))
            types(S(nxt, 16, 80), S("ps_c1", 0, 64))
            effects(5, 8, nxt, 0, True)
            effects(0, 5, nxt, 1, False)
        else:
            leaving(16, "rotate out")
            act(S("fin", 80, 128), S("ps_c0", 64, 112), Fn.Identity, bias=float(EMPTY), scale=-1.0)
            act(S("fin", 0, 16), S("ps_v1", 0, 16), Fn.Copy)
            types(S("fin", 16, 80), S("ps_c1", 0, 64))
            dmas("y", "yp out", [(D("pst", 0, N), S("fin", 0, 128))])
            dmas("s", "yp own", [(T.yp[blk(r), :], S("fin", 0, 128, p=blk(r)))])
            exchange("pst", "pld", "ap")
            dmas("y", "yp in", [(T.yp[B * a:B * b, :], D("pld", a, b)) for a, b in ((0, r), (r + 1, N)) if a < b])
    issue_all()
    for sem in count:
        g.wait_ge(T.sem[sem], count[sem])
